import numpy as np
import ml_dtypes


def mxq(x, axis, fmt="e4m3"):
    dtype, down = {"e4m3": (ml_dtypes.float8_e4m3fn, 7), "e5m2": (ml_dtypes.float8_e5m2, 14)}[fmt]
    v = np.moveaxis(np.asarray(x, np.float32).astype(ml_dtypes.bfloat16).astype(np.float64), axis, -1)
    blocks = v.reshape(v.shape[:-1] + (-1, 32))
    amax = np.abs(blocks).max(-1, keepdims=True)
    byte = np.maximum(np.where(amax > 0, np.frexp(amax)[1] - 1 + 127, 0) - down, 1)
    scale = np.exp2(byte - 127.0)
    codes = (blocks / scale).astype(np.float32).astype(dtype).astype(np.float64)
    return np.moveaxis((codes * scale).reshape(v.shape), -1, axis)


WIDE = False


def mx_kscale(k):
    if not WIDE:
        return np.ones(k)
    levels = np.array([10, -10, 5, -5, 0])
    if k % 512:
        return np.exp2(np.random.permutation(np.resize(levels, k // 32))).repeat(32)
    a = np.empty((k // 512, 16))
    for p in range(k // 512):
        a[p, :8] = np.random.permutation(np.resize(levels, 8))
        for g in range(8):
            far = levels[np.abs(levels - a[p, g]) >= 10]
            a[p, g + 8] = far[np.random.randint(len(far))]
    return np.exp2(a.ravel()).repeat(32)


def f64(x):
    return np.asarray(x).astype(np.float64)


def striped(idx):
    return np.tile(idx.reshape(-1, 16).T, (8, 1)).astype(np.uint16)


def unstriped(offs):
    return offs[:16].T.reshape(-1).astype(np.int64)


def pack_weight(w):
    k, n = w.shape
    w = f64(np.asarray(w, np.float32).astype(ml_dtypes.bfloat16)).reshape(k // 32, 32, n)
    amax = np.abs(w).max(1)
    byte = np.clip(np.where(amax > 0, np.frexp(amax)[1] - 1 + 127 - 7, 1), 1, 254)
    scaled = (w * np.exp2(127.0 - byte)[:, None, :]).reshape(k, n).astype(np.float32)
    words = np.ascontiguousarray(scaled.reshape(k // 512, 128, 4, n).transpose(0, 1, 3, 2)).astype(ml_dtypes.float8_e4m3fn).view(np.uint8)
    return words, np.ascontiguousarray(byte.astype(np.uint8).reshape(k // 512, 16, n))


def unpack_weight(words, scales):
    g, p, n, _ = words.shape
    vals = np.ascontiguousarray(words).view(ml_dtypes.float8_e4m3fn).astype(np.float64) * np.repeat(np.exp2(scales.astype(np.float64) - 127.0), 8, axis=1)[..., None]
    return vals.transpose(0, 1, 3, 2).reshape(g * 512, n)


K, T, S, J = 1024, 2048, 512, 512


def setup_inputs():
    n = np.random.standard_normal
    s = mx_kscale(K)[:, None]
    packed_xT = pack_weight(n((K, T)) * s)
    return {
        "x_words": packed_xT[0],
        "x_scales": packed_xT[1],
        "hT": (n((K, J)) / np.sqrt(K) / s).astype(np.float32),
        "label": (np.random.uniform(0.0, 0.4, (J, S))).astype(np.float32),
        "offs": striped(np.random.permutation(T)[:S]),
    }


def reference(x_words, x_scales, hT, label, offs):
    hTq = mxq(f64(hT), 0, "e4m3")
    xq = unpack_weight(x_words, x_scales)[:, unstriped(offs)]
    z = 4.0 * ((hTq.T @ xq) - f64(label))
    e = np.exp(z - z.max(axis=1, keepdims=True))
    return e / e.sum(axis=1, keepdims=True)

@@ -1,0 +1,167 @@
+from contextlib import ExitStack
+
+import concourse.mybir as mybir
+
+K, T, S, J = 1024, 2048, 512, 512
+P = 128
+PACK = 4
+K_PASS = P * PACK
+PASSES = K // K_PASS
+TILES = J // P
+SCALE = 4.0
+FLOPS = 2 * K * J * S
+
+F32 = mybir.dt.float32
+BF16 = mybir.dt.bfloat16
+I32 = mybir.dt.int32
+U32 = mybir.dt.uint32
+U16 = mybir.dt.uint16
+U8 = mybir.dt.uint8
+FP8X4 = mybir.dt.float8_e4m3fn_x4
+ALU = mybir.AluOpType
+ACT = mybir.ActivationFunctionType
+
+
+def tile_picked_zams_soft_p_kernel(tc, x_words, x_scales, hT, label, offs, out):
+    nc = tc.nc
+    with ExitStack() as ctx:
+        keep = ctx.enter_context(tc.tile_pool(name="keep", bufs=1))
+        psum = ctx.enter_context(tc.psum_pool(name="psum", bufs=1))
+
+        offsets = keep.tile([P, S // 16], U16, name="offsets")
+        scale_table = keep.tile([P, T], U8, name="scale_table", align_bytes=64)
+        word_table = [keep.tile([P, T], I32, name="word_table%d" % o, align_bytes=64) for o in range(PASSES)]
+        h_raw = [[keep.tile([P, PACK, P], F32, name="h_raw%d_%d" % (m, o)) for o in range(PASSES)] for m in range(TILES)]
+        margin = [keep.tile([P, S], F32, name="margin%d" % m) for m in range(TILES)]
+
+        nc.vector.memset(scale_table[:].bitcast(I32), 0)
+        warm_in = keep.tile([P, 1], F32, name="warm_in")
+        warm_out = keep.tile([P, 1], F32, name="warm_out")
+        nc.vector.memset(warm_in[:], 0.0)
+        nc.scalar.activation(warm_out[:], warm_in[:], ACT.Exp)
+
+        def load_words(o):
+            nc.sync.dma_start(out=word_table[o][:], in_=x_words[o].rearrange("p n t -> p (n t)").bitcast(I32))
+
+        def load_h(m, o):
+            rows = hT[o * K_PASS : (o + 1) * K_PASS, m * P : (m + 1) * P]
+            nc.sync.dma_start(out=h_raw[m][o][:], in_=rows.rearrange("(p j) c -> p j c", j=PACK))
+
+        def load_margin(m):
+            nc.sync.dma_start(out=margin[m][:], in_=label[m * P : (m + 1) * P, :])
+
+        load_words(0)
+        nc.sync.dma_start(offsets[:], offs)
+        for q in range(4):
+            nc.sync.dma_start(
+                out=scale_table[32 * q : 32 * q + 4 * PASSES, :].bitcast(I32),
+                in_=x_scales[:, 4 * q : 4 * q + 4, :].bitcast(I32),
+            )
+        load_h(0, 0)
+        load_h(0, 1)
+        load_words(1)
+        load_h(1, 0)
+        load_h(1, 1)
+        load_h(2, 0)
+        load_margin(0)
+        load_h(2, 1)
+        load_h(3, 0)
+        load_margin(1)
+        load_h(3, 1)
+        load_margin(2)
+        load_margin(3)
+
+        x_codes = [keep.tile([P, S], U32, name="x_codes%d" % o, align_bytes=64) for o in range(PASSES)]
+        x_planes = keep.tile([P, S], U8, name="x_planes", align_bytes=64)
+        scores = [psum.tile([P, S], F32, name="scores%d" % m) for m in range(TILES)]
+        grouped = [[keep.tile([P, P, PACK], BF16, name="grouped%d_%d" % (m, o), align_bytes=64) for o in range(PASSES)] for m in range(TILES)]
+        h_codes = [[keep.tile([P, P], U32, name="h_codes%d_%d" % (m, o), align_bytes=64) for o in range(PASSES)] for m in range(TILES)]
+        h_plane = [[keep.tile([P, P], U8, name="h_plane%d_%d" % (m, o), align_bytes=64) for o in range(PASSES)] for m in range(TILES)]
+        neg = [keep.tile([P, S], F32, name="neg%d" % m) for m in range(TILES)]
+        e = [keep.tile([P, S], F32, name="e%d" % m) for m in range(TILES)]
+        prob = [keep.tile([P, S], F32, name="prob%d" % m) for m in range(TILES)]
+        low = [keep.tile([P, 1], F32, name="low%d" % m) for m in range(TILES)]
+        total = [keep.tile([P, 1], F32, name="total%d" % m) for m in range(TILES)]
+        inv = [keep.tile([P, 1], F32, name="inv%d" % m) for m in range(TILES)]
+
+        def gather_words(o):
+            nc.vector.tensor_copy(x_codes[o][:], word_table[o][:].bitcast(U32).indirect(offsets[:]))
+
+        def interleave(m, o):
+            nc.scalar.activation(grouped[m][o][:], h_raw[m][o][:].rearrange("p j c -> p c j"), ACT.Copy, scale=SCALE)
+
+        def quantize(m, o):
+            nc.vector.quantize_mx(
+                out=h_codes[m][o][:].bitcast(FP8X4),
+                scales=h_plane[m][o][:],
+                in_=grouped[m][o][:].rearrange("p c j -> p (c j)"),
+            )
+
+        def multiply(m, o):
+            nc.tensor.matmul_mx(
+                out=scores[m][:],
+                lhsT=h_codes[m][o][:].bitcast(FP8X4),
+                lhsT_scale=h_plane[m][o][:],
+                rhs=x_codes[o][:].bitcast(FP8X4),
+                rhs_scale=x_planes[4 * o :, :],
+                start=(o == 0),
+                stop=(o == PASSES - 1),
+            )
+
+        def prepare(m, o):
+            interleave(m, o)
+            quantize(m, o)
+            multiply(m, o)
+
+        def subtract(m):
+            nc.vector.scalar_tensor_tensor(neg[m][:], margin[m][:], SCALE, scores[m][:], ALU.mult, ALU.subtract)
+
+        def lowest(m):
+            nc.vector.tensor_reduce(low[m][:], neg[m][:], mybir.AxisListType.X, ALU.min)
+
+        def exponent(m):
+            nc.scalar.activation(e[m][:], neg[m][:], ACT.Exp, bias=low[m][:], scale=-1.0, accum_out=total[m][:])
+
+        def invert(m):
+            nc.vector.reciprocal(inv[m][:], total[m][:])
+
+        def finish(m, on_scalar):
+            if on_scalar:
+                nc.scalar.activation(prob[m][:], e[m][:], ACT.Copy, scale=inv[m][:])
+            else:
+                nc.vector.tensor_scalar(prob[m][:], e[m][:], inv[m][:], None, ALU.mult)
+            nc.sync.dma_start(out=out[m * P : (m + 1) * P, :], in_=prob[m][:])
+
+        gather_words(0)
+        nc.vector.tensor_copy(x_planes[:], scale_table[:].indirect(offsets[:]))
+        prepare(0, 0)
+        interleave(0, 1)
+        quantize(0, 1)
+        gather_words(1)
+        multiply(0, 1)
+        prepare(1, 0)
+        prepare(1, 1)
+        subtract(0)
+        prepare(2, 0)
+        lowest(0)
+        prepare(2, 1)
+        exponent(0)
+        subtract(1)
+        invert(0)
+        prepare(3, 0)
+        lowest(1)
+        finish(0, True)
+        prepare(3, 1)
+        exponent(1)
+        subtract(2)
+        invert(1)
+        lowest(2)
+        finish(1, True)
+        exponent(2)
+        subtract(3)
+        invert(2)
+        lowest(3)
+        finish(2, False)
+        exponent(3)
+        invert(3)
+        finish(3, False)

@@ -8,7 +8,12 @@ PACK = 4
 K_PASS = P * PACK
 PASSES = K // K_PASS
 TILES = J // P
+QUADRANTS = 4
+QUADRANT = P // QUADRANTS
+PLANE_ROWS = 4
+LIST_ROWS = 16
 SCALE = 4.0
+AHEAD = 2
 FLOPS = 2 * K * J * S
 
 F32 = mybir.dt.float32
@@ -28,17 +33,13 @@ def tile_picked_zams_soft_p_kernel(tc, x_words, x_scales, hT, label, offs, out):
         keep = ctx.enter_context(tc.tile_pool(name="keep", bufs=1))
         psum = ctx.enter_context(tc.psum_pool(name="psum", bufs=1))
 
-        offsets = keep.tile([P, S // 16], U16, name="offsets")
+        offsets = keep.tile([P, S // LIST_ROWS], U16, name="offsets")
         scale_table = keep.tile([P, T], U8, name="scale_table", align_bytes=64)
         word_table = [keep.tile([P, T], I32, name="word_table%d" % o, align_bytes=64) for o in range(PASSES)]
         h_raw = [[keep.tile([P, PACK, P], F32, name="h_raw%d_%d" % (m, o)) for o in range(PASSES)] for m in range(TILES)]
         margin = [keep.tile([P, S], F32, name="margin%d" % m) for m in range(TILES)]
 
         nc.vector.memset(scale_table[:].bitcast(I32), 0)
-        warm_in = keep.tile([P, 1], F32, name="warm_in")
-        warm_out = keep.tile([P, 1], F32, name="warm_out")
-        nc.vector.memset(warm_in[:], 0.0)
-        nc.scalar.activation(warm_out[:], warm_in[:], ACT.Exp)
 
         def load_words(o):
             nc.sync.dma_start(out=word_table[o][:], in_=x_words[o].rearrange("p n t -> p (n t)").bitcast(I32))
@@ -52,24 +53,21 @@ def tile_picked_zams_soft_p_kernel(tc, x_words, x_scales, hT, label, offs, out):
 
         load_words(0)
         nc.sync.dma_start(offsets[:], offs)
-        for q in range(4):
+        for q in range(QUADRANTS):
             nc.sync.dma_start(
-                out=scale_table[32 * q : 32 * q + 4 * PASSES, :].bitcast(I32),
-                in_=x_scales[:, 4 * q : 4 * q + 4, :].bitcast(I32),
+                out=scale_table[QUADRANT * q : QUADRANT * q + PLANE_ROWS * PASSES, :].bitcast(I32),
+                in_=x_scales[:, PLANE_ROWS * q : PLANE_ROWS * (q + 1), :].bitcast(I32),
             )
         load_h(0, 0)
         load_h(0, 1)
         load_words(1)
-        load_h(1, 0)
-        load_h(1, 1)
-        load_h(2, 0)
-        load_margin(0)
-        load_h(2, 1)
-        load_h(3, 0)
-        load_margin(1)
-        load_h(3, 1)
-        load_margin(2)
-        load_margin(3)
+        for m in range(1, TILES):
+            load_h(m, 0)
+            if m >= AHEAD:
+                load_margin(m - AHEAD)
+            load_h(m, 1)
+        for m in range(TILES - AHEAD, TILES):
+            load_margin(m)
 
         x_codes = [keep.tile([P, S], U32, name="x_codes%d" % o, align_bytes=64) for o in range(PASSES)]
         x_planes = keep.tile([P, S], U8, name="x_planes", align_bytes=64)
@@ -103,7 +101,7 @@ def tile_picked_zams_soft_p_kernel(tc, x_words, x_scales, hT, label, offs, out):
                 lhsT=h_codes[m][o][:].bitcast(FP8X4),
                 lhsT_scale=h_plane[m][o][:],
                 rhs=x_codes[o][:].bitcast(FP8X4),
-                rhs_scale=x_planes[4 * o :, :],
+                rhs_scale=x_planes[PLANE_ROWS * o :, :],
                 start=(o == 0),
                 stop=(o == PASSES - 1),
             )
@@ -125,8 +123,8 @@ def tile_picked_zams_soft_p_kernel(tc, x_words, x_scales, hT, label, offs, out):
         def invert(m):
             nc.vector.reciprocal(inv[m][:], total[m][:])
 
-        def finish(m, on_scalar):
-            if on_scalar:
+        def finish(m):
+            if m < TILES - AHEAD:
                 nc.scalar.activation(prob[m][:], e[m][:], ACT.Copy, scale=inv[m][:])
             else:
                 nc.vector.tensor_scalar(prob[m][:], e[m][:], inv[m][:], None, ALU.mult)
@@ -141,27 +139,18 @@ def tile_picked_zams_soft_p_kernel(tc, x_words, x_scales, hT, label, offs, out):
         multiply(0, 1)
         prepare(1, 0)
         prepare(1, 1)
-        subtract(0)
-        prepare(2, 0)
-        lowest(0)
-        prepare(2, 1)
-        exponent(0)
-        subtract(1)
-        invert(0)
-        prepare(3, 0)
-        lowest(1)
-        finish(0, True)
-        prepare(3, 1)
-        exponent(1)
-        subtract(2)
-        invert(1)
-        lowest(2)
-        finish(1, True)
-        exponent(2)
-        subtract(3)
-        invert(2)
-        lowest(3)
-        finish(2, False)
-        exponent(3)
-        invert(3)
-        finish(3, False)
+
+        for m in range(TILES):
+            subtract(m)
+            if m > 0:
+                invert(m - 1)
+            if m + AHEAD < TILES:
+                prepare(m + AHEAD, 0)
+            lowest(m)
+            if m > 0:
+                finish(m - 1)
+            if m + AHEAD < TILES:
+                prepare(m + AHEAD, 1)
+            exponent(m)
+        invert(TILES - 1)
+        finish(TILES - 1)

@@ -35,47 +35,55 @@ def tile_picked_zams_soft_p_kernel(tc, x_words, x_scales, hT, label, offs, out):
 
         offsets = keep.tile([P, S // LIST_ROWS], U16, name="offsets")
         scale_table = keep.tile([P, T], U8, name="scale_table", align_bytes=64)
-        word_table = [keep.tile([P, T], I32, name="word_table%d" % o, align_bytes=64) for o in range(PASSES)]
-        h_raw = [[keep.tile([P, PACK, P], F32, name="h_raw%d_%d" % (m, o)) for o in range(PASSES)] for m in range(TILES)]
-        margin = [keep.tile([P, S], F32, name="margin%d" % m) for m in range(TILES)]
+        word_table = [keep.tile([P, T], I32, name="word_table%d" % o, tag="words%d" % o, align_bytes=64) for o in range(PASSES)]
+        h_first = keep.tile([P, PACK, J], F32, name="h_first", tag="first", align_bytes=64)
+        h_last = [keep.tile([P, PACK, 2 * P], F32, name="h_last%d" % u, tag="last%d" % u, align_bytes=64) for u in range(TILES // 2)]
+        margin = [keep.tile([P, S], F32, name="margin%d" % m, tag="margin%d" % m, align_bytes=64) for m in range(TILES)]
 
         nc.vector.memset(scale_table[:].bitcast(I32), 0)
 
         def load_words(o):
             nc.sync.dma_start(out=word_table[o][:], in_=x_words[o].rearrange("p n t -> p (n t)").bitcast(I32))
 
-        def load_h(m, o):
-            rows = hT[o * K_PASS : (o + 1) * K_PASS, m * P : (m + 1) * P]
-            nc.sync.dma_start(out=h_raw[m][o][:], in_=rows.rearrange("(p j) c -> p j c", j=PACK))
+        def load_h(dst, o, faces):
+            rows = hT[o * K_PASS : (o + 1) * K_PASS, faces]
+            nc.sync.dma_start(out=dst[:], in_=rows.rearrange("(p j) c -> p j c", j=PACK))
+
+        def load_last(u):
+            load_h(h_last[u], 1, slice(2 * u * P, 2 * (u + 1) * P))
 
         def load_margin(m):
             nc.sync.dma_start(out=margin[m][:], in_=label[m * P : (m + 1) * P, :])
 
-        load_words(0)
+        load_h(h_first, 0, slice(0, J))
         nc.sync.dma_start(offsets[:], offs)
         for q in range(QUADRANTS):
             nc.sync.dma_start(
                 out=scale_table[QUADRANT * q : QUADRANT * q + PLANE_ROWS * PASSES, :].bitcast(I32),
                 in_=x_scales[:, PLANE_ROWS * q : PLANE_ROWS * (q + 1), :].bitcast(I32),
             )
-        load_h(0, 0)
-        load_h(0, 1)
+        load_words(0)
+        load_last(0)
         load_words(1)
-        for m in range(1, TILES):
-            load_h(m, 0)
-            if m >= AHEAD:
-                load_margin(m - AHEAD)
-            load_h(m, 1)
-        for m in range(TILES - AHEAD, TILES):
+        load_last(1)
+        for m in range(TILES):
             load_margin(m)
 
-        x_codes = [keep.tile([P, S], U32, name="x_codes%d" % o, align_bytes=64) for o in range(PASSES)]
+        x_codes = [keep.tile([P, S], U32, name="x_codes%d" % o, tag=("first", "last0")[o], align_bytes=64) for o in range(PASSES)]
         x_planes = keep.tile([P, S], U8, name="x_planes", align_bytes=64)
         scores = [psum.tile([P, S], F32, name="scores%d" % m) for m in range(TILES)]
-        grouped = [[keep.tile([P, P, PACK], BF16, name="grouped%d_%d" % (m, o), align_bytes=64) for o in range(PASSES)] for m in range(TILES)]
-        h_codes = [[keep.tile([P, P], U32, name="h_codes%d_%d" % (m, o), align_bytes=64) for o in range(PASSES)] for m in range(TILES)]
+        neg = [keep.tile([P, S], F32, name="neg%d" % m, align_bytes=64) for m in range(TILES)]
+        stage = [keep.tile([P, P * PACK], BF16, name="stage%d" % m, align_bytes=64) for m in range(TILES)]
+        grouped = [[stage[m][:], stage[m][:]] for m in range(TILES)]
+        last_tag = ["words0", "codes1", "words1", "margin0"]
+        h_codes = [
+            [
+                keep.tile([P, P], U32, name="h_codes%d_0" % m, align_bytes=64),
+                keep.tile([P, P], U32, name="h_codes%d_1" % m, tag=last_tag[m], align_bytes=64),
+            ]
+            for m in range(TILES)
+        ]
         h_plane = [[keep.tile([P, P], U8, name="h_plane%d_%d" % (m, o), align_bytes=64) for o in range(PASSES)] for m in range(TILES)]
-        neg = [keep.tile([P, S], F32, name="neg%d" % m) for m in range(TILES)]
         e = [keep.tile([P, S], F32, name="e%d" % m) for m in range(TILES)]
         prob = [keep.tile([P, S], F32, name="prob%d" % m) for m in range(TILES)]
         low = [keep.tile([P, 1], F32, name="low%d" % m) for m in range(TILES)]
@@ -86,13 +94,19 @@ def tile_picked_zams_soft_p_kernel(tc, x_words, x_scales, hT, label, offs, out):
             nc.vector.tensor_copy(x_codes[o][:], word_table[o][:].bitcast(U32).indirect(offsets[:]))
 
         def interleave(m, o):
-            nc.scalar.activation(grouped[m][o][:], h_raw[m][o][:].rearrange("p j c -> p c j"), ACT.Copy, scale=SCALE)
+            raw = h_first[:, :, m * P : (m + 1) * P] if o == 0 else h_last[m // 2][:, :, (m % 2) * P : (m % 2 + 1) * P]
+            nc.scalar.activation(
+                grouped[m][o].rearrange("p (c i j) -> p c j i", i=PACK, j=PACK),
+                raw.rearrange("p j (c i) -> p c j i", i=PACK),
+                ACT.Copy,
+                scale=SCALE,
+            )
 
         def quantize(m, o):
             nc.vector.quantize_mx(
                 out=h_codes[m][o][:].bitcast(FP8X4),
                 scales=h_plane[m][o][:],
-                in_=grouped[m][o][:].rearrange("p c j -> p (c j)"),
+                in_=grouped[m][o],
             )
 
         def multiply(m, o):
@@ -130,27 +144,33 @@ def tile_picked_zams_soft_p_kernel(tc, x_words, x_scales, hT, label, offs, out):
                 nc.vector.tensor_scalar(prob[m][:], e[m][:], inv[m][:], None, ALU.mult)
             nc.sync.dma_start(out=out[m * P : (m + 1) * P, :], in_=prob[m][:])
 
-        gather_words(0)
+        for m in range(TILES):
+            interleave(m, 0)
         nc.vector.tensor_copy(x_planes[:], scale_table[:].indirect(offsets[:]))
-        prepare(0, 0)
-        interleave(0, 1)
-        quantize(0, 1)
+        for m in range(TILES):
+            quantize(m, 0)
+        gather_words(0)
+        for m in range(TILES):
+            multiply(m, 0)
+        for m in range(AHEAD):
+            interleave(m, 1)
+            quantize(m, 1)
         gather_words(1)
-        multiply(0, 1)
-        prepare(1, 0)
-        prepare(1, 1)
+        for m in range(AHEAD):
+            multiply(m, 1)
+        prepare(AHEAD, 1)
+        interleave(TILES - 1, 1)
 
         for m in range(TILES):
             subtract(m)
+            if m == 0:
+                quantize(TILES - 1, 1)
+                multiply(TILES - 1, 1)
             if m > 0:
                 invert(m - 1)
-            if m + AHEAD < TILES:
-                prepare(m + AHEAD, 0)
             lowest(m)
+            exponent(m)
             if m > 0:
                 finish(m - 1)
-            if m + AHEAD < TILES:
-                prepare(m + AHEAD, 1)
-            exponent(m)
         invert(TILES - 1)
         finish(TILES - 1)

@@ -75,15 +75,19 @@ def tile_picked_zams_soft_p_kernel(tc, x_words, x_scales, hT, label, offs, out):
         neg = [keep.tile([P, S], F32, name="neg%d" % m, align_bytes=64) for m in range(TILES)]
         stage = [keep.tile([P, P * PACK], BF16, name="stage%d" % m, align_bytes=64) for m in range(TILES)]
         grouped = [[stage[m][:], stage[m][:]] for m in range(TILES)]
-        last_tag = ["words0", "codes1", "words1", "margin0"]
-        h_codes = [
-            [
-                keep.tile([P, P], U32, name="h_codes%d_0" % m, align_bytes=64),
-                keep.tile([P, P], U32, name="h_codes%d_1" % m, tag=last_tag[m], align_bytes=64),
-            ]
-            for m in range(TILES)
-        ]
-        h_plane = [[keep.tile([P, P], U8, name="h_plane%d_%d" % (m, o), align_bytes=64) for o in range(PASSES)] for m in range(TILES)]
+        last_tag = ["words0", "codes1"]
+        h_codes = [[keep.tile([P, P], U32, name="h_codes%d_0" % m, align_bytes=64)[:]] for m in range(TILES)]
+        h_plane = [[keep.tile([P, P], U8, name="h_plane%d_0" % m, align_bytes=64)[:]] for m in range(TILES)]
+        for m in range(2):
+            h_codes[m].append(keep.tile([P, P], U32, name="h_codes%d_1" % m, tag=last_tag[m], align_bytes=64)[:])
+            h_plane[m].append(keep.tile([P, P], U8, name="h_plane%d_1" % m, align_bytes=64)[:])
+        late_stage = keep.tile([P, 2 * P * PACK], BF16, name="late_stage", align_bytes=64)
+        late_codes = keep.tile([P, 2 * P], U32, name="late_codes", tag="margin0", align_bytes=64)
+        late_plane = keep.tile([P, 2 * P], U8, name="late_plane", align_bytes=64)
+        for m in range(2):
+            grouped[m + 2][1] = late_stage[:, m * P * PACK : (m + 1) * P * PACK]
+            h_codes[m + 2].append(late_codes[:, m * P : (m + 1) * P])
+            h_plane[m + 2].append(late_plane[:, m * P : (m + 1) * P])
         e = [keep.tile([P, S], F32, name="e%d" % m) for m in range(TILES)]
         prob = [keep.tile([P, S], F32, name="prob%d" % m) for m in range(TILES)]
         low = [keep.tile([P, 1], F32, name="low%d" % m) for m in range(TILES)]
@@ -104,16 +108,16 @@ def tile_picked_zams_soft_p_kernel(tc, x_words, x_scales, hT, label, offs, out):
 
         def quantize(m, o):
             nc.vector.quantize_mx(
-                out=h_codes[m][o][:].bitcast(FP8X4),
-                scales=h_plane[m][o][:],
+                out=h_codes[m][o].bitcast(FP8X4),
+                scales=h_plane[m][o],
                 in_=grouped[m][o],
             )
 
         def multiply(m, o):
             nc.tensor.matmul_mx(
                 out=scores[m][:],
-                lhsT=h_codes[m][o][:].bitcast(FP8X4),
-                lhsT_scale=h_plane[m][o][:],
+                lhsT=h_codes[m][o].bitcast(FP8X4),
+                lhsT_scale=h_plane[m][o],
                 rhs=x_codes[o][:].bitcast(FP8X4),
                 rhs_scale=x_planes[PLANE_ROWS * o :, :],
                 start=(o == 0),
@@ -138,8 +142,10 @@ def tile_picked_zams_soft_p_kernel(tc, x_words, x_scales, hT, label, offs, out):
             nc.vector.reciprocal(inv[m][:], total[m][:])
 
         def finish(m):
-            if m < TILES - AHEAD:
+            if m == 0:
                 nc.scalar.activation(prob[m][:], e[m][:], ACT.Copy, scale=inv[m][:])
+            elif m == 1:
+                nc.gpsimd.tensor_scalar(prob[m][:], e[m][:], inv[m][:], 0.0, ALU.mult, ALU.add)
             else:
                 nc.vector.tensor_scalar(prob[m][:], e[m][:], inv[m][:], None, ALU.mult)
             nc.sync.dma_start(out=out[m * P : (m + 1) * P, :], in_=prob[m][:])
@@ -158,19 +164,24 @@ def tile_picked_zams_soft_p_kernel(tc, x_words, x_scales, hT, label, offs, out):
         gather_words(1)
         for m in range(AHEAD):
             multiply(m, 1)
-        prepare(AHEAD, 1)
-        interleave(TILES - 1, 1)
+        interleave(2, 1)
+        interleave(3, 1)
 
-        for m in range(TILES):
-            subtract(m)
-            if m == 0:
-                quantize(TILES - 1, 1)
-                multiply(TILES - 1, 1)
-            if m > 0:
-                invert(m - 1)
+        subtract(0)
+        subtract(1)
+        nc.vector.quantize_mx(out=late_codes[:].bitcast(FP8X4), scales=late_plane[:], in_=late_stage[:])
+        multiply(2, 1)
+        multiply(3, 1)
+        for m in range(2):
             lowest(m)
             exponent(m)
-            if m > 0:
-                finish(m - 1)
-        invert(TILES - 1)
-        finish(TILES - 1)
+        for m in range(2):
+            subtract(m + 2)
+            invert(m)
+            finish(m)
+        for m in range(2, TILES):
+            lowest(m)
+            exponent(m)
+        for m in range(2, TILES):
+            invert(m)
+            finish(m)

@@ -63,19 +63,21 @@ def tile_picked_zams_soft_p_kernel(tc, x_words, x_scales, hT, label, offs, out):
                 in_=x_scales[:, PLANE_ROWS * q : PLANE_ROWS * (q + 1), :].bitcast(I32),
             )
         load_words(0)
-        load_last(0)
         load_words(1)
+        load_last(0)
         load_last(1)
         for m in range(TILES):
             load_margin(m)
 
-        x_codes = [keep.tile([P, S], U32, name="x_codes%d" % o, tag=("first", "last0")[o], align_bytes=64) for o in range(PASSES)]
+        x_codes = [keep.tile([P, S], U32, name="x_codes%d" % o, tag=("first", "words0")[o], align_bytes=64) for o in range(PASSES)]
         x_planes = keep.tile([P, S], U8, name="x_planes", align_bytes=64)
         scores = [psum.tile([P, S], F32, name="scores%d" % m) for m in range(TILES)]
         neg = [keep.tile([P, S], F32, name="neg%d" % m, align_bytes=64) for m in range(TILES)]
         stage = [keep.tile([P, P * PACK], BF16, name="stage%d" % m, align_bytes=64) for m in range(TILES)]
         grouped = [[stage[m][:], stage[m][:]] for m in range(TILES)]
-        last_tag = ["words0", "codes1"]
+        lead = keep.tile([P, P * PACK], BF16, name="lead", tag="words1", align_bytes=64)
+        grouped[0][1] = lead[:]
+        last_tag = ["codes0", "codes1"]
         h_codes = [[keep.tile([P, P], U32, name="h_codes%d_0" % m, align_bytes=64)[:]] for m in range(TILES)]
         h_plane = [[keep.tile([P, P], U8, name="h_plane%d_0" % m, align_bytes=64)[:]] for m in range(TILES)]
         for m in range(2):
@@ -99,12 +101,12 @@ def tile_picked_zams_soft_p_kernel(tc, x_words, x_scales, hT, label, offs, out):
 
         def interleave(m, o):
             raw = h_first[:, :, m * P : (m + 1) * P] if o == 0 else h_last[m // 2][:, :, (m % 2) * P : (m % 2 + 1) * P]
-            nc.scalar.activation(
-                grouped[m][o].rearrange("p (c i j) -> p c j i", i=PACK, j=PACK),
-                raw.rearrange("p j (c i) -> p c j i", i=PACK),
-                ACT.Copy,
-                scale=SCALE,
-            )
+            dst = grouped[m][o].rearrange("p (c i j) -> p c j i", i=PACK, j=PACK)
+            src = raw.rearrange("p j (c i) -> p c j i", i=PACK)
+            if (m, o) == (0, 1):
+                nc.vector.tensor_scalar(dst, src, SCALE, None, ALU.mult)
+            else:
+                nc.scalar.activation(dst, src, ACT.Copy, scale=SCALE)
 
         def quantize(m, o):
             nc.vector.quantize_mx(
@@ -158,12 +160,9 @@ def tile_picked_zams_soft_p_kernel(tc, x_words, x_scales, hT, label, offs, out):
         gather_words(0)
         for m in range(TILES):
             multiply(m, 0)
-        for m in range(AHEAD):
-            interleave(m, 1)
-            quantize(m, 1)
         gather_words(1)
         for m in range(AHEAD):
-            multiply(m, 1)
+            prepare(m, 1)
         interleave(2, 1)
         interleave(3, 1)
 

@@ -29,6 +29,8 @@ ACT = mybir.ActivationFunctionType
 
 def tile_picked_zams_soft_p_kernel(tc, x_words, x_scales, hT, label, offs, out):
     nc = tc.nc
+    HALF = S // 2
+    PAIR = 2 * P
     with ExitStack() as ctx:
         keep = ctx.enter_context(tc.tile_pool(name="keep", bufs=1))
         psum = ctx.enter_context(tc.psum_pool(name="psum", bufs=1))
@@ -36,26 +38,19 @@ def tile_picked_zams_soft_p_kernel(tc, x_words, x_scales, hT, label, offs, out):
         offsets = keep.tile([P, S // LIST_ROWS], U16, name="offsets")
         scale_table = keep.tile([P, T], U8, name="scale_table", align_bytes=64)
         word_table = [keep.tile([P, T], I32, name="word_table%d" % o, tag="words%d" % o, align_bytes=64) for o in range(PASSES)]
-        h_first = keep.tile([P, PACK, J], F32, name="h_first", tag="first", align_bytes=64)
-        h_last = [keep.tile([P, PACK, 2 * P], F32, name="h_last%d" % u, tag="last%d" % u, align_bytes=64) for u in range(TILES // 2)]
-        margin = [keep.tile([P, S], F32, name="margin%d" % m, tag="margin%d" % m, align_bytes=64) for m in range(TILES)]
+        h_raw = [keep.tile([P, PACK, J], F32, name="h_raw%d" % o, align_bytes=64) for o in range(PASSES)]
+        margin = [keep.tile([P, S], F32, name="margin%d" % m, align_bytes=64) for m in range(TILES)]
 
         nc.vector.memset(scale_table[:].bitcast(I32), 0)
 
         def load_words(o):
             nc.sync.dma_start(out=word_table[o][:], in_=x_words[o].rearrange("p n t -> p (n t)").bitcast(I32))
 
-        def load_h(dst, o, faces):
-            rows = hT[o * K_PASS : (o + 1) * K_PASS, faces]
-            nc.sync.dma_start(out=dst[:], in_=rows.rearrange("(p j) c -> p j c", j=PACK))
+        def load_h(o):
+            rows = hT[o * K_PASS : (o + 1) * K_PASS, :]
+            nc.sync.dma_start(out=h_raw[o][:], in_=rows.rearrange("(p j) c -> p j c", j=PACK))
 
-        def load_last(u):
-            load_h(h_last[u], 1, slice(2 * u * P, 2 * (u + 1) * P))
-
-        def load_margin(m):
-            nc.sync.dma_start(out=margin[m][:], in_=label[m * P : (m + 1) * P, :])
-
-        load_h(h_first, 0, slice(0, J))
+        load_h(0)
         nc.sync.dma_start(offsets[:], offs)
         for q in range(QUADRANTS):
             nc.sync.dma_start(
@@ -63,79 +58,66 @@ def tile_picked_zams_soft_p_kernel(tc, x_words, x_scales, hT, label, offs, out):
                 in_=x_scales[:, PLANE_ROWS * q : PLANE_ROWS * (q + 1), :].bitcast(I32),
             )
         load_words(0)
+        load_h(1)
         load_words(1)
-        load_last(0)
-        load_last(1)
         for m in range(TILES):
-            load_margin(m)
+            nc.sync.dma_start(out=margin[m][:], in_=label[m * P : (m + 1) * P, :])
 
-        x_codes = [keep.tile([P, S], U32, name="x_codes%d" % o, tag=("first", "words0")[o], align_bytes=64) for o in range(PASSES)]
-        x_planes = keep.tile([P, S], U8, name="x_planes", align_bytes=64)
-        scores = [psum.tile([P, S], F32, name="scores%d" % m) for m in range(TILES)]
-        neg = [keep.tile([P, S], F32, name="neg%d" % m, align_bytes=64) for m in range(TILES)]
-        stage = [keep.tile([P, P * PACK], BF16, name="stage%d" % m, align_bytes=64) for m in range(TILES)]
-        grouped = [[stage[m][:], stage[m][:]] for m in range(TILES)]
-        lead = keep.tile([P, P * PACK], BF16, name="lead", tag="words1", align_bytes=64)
-        grouped[0][1] = lead[:]
-        last_tag = ["codes0", "codes1"]
-        h_codes = [[keep.tile([P, P], U32, name="h_codes%d_0" % m, align_bytes=64)[:]] for m in range(TILES)]
-        h_plane = [[keep.tile([P, P], U8, name="h_plane%d_0" % m, align_bytes=64)[:]] for m in range(TILES)]
-        for m in range(2):
-            h_codes[m].append(keep.tile([P, P], U32, name="h_codes%d_1" % m, tag=last_tag[m], align_bytes=64)[:])
-            h_plane[m].append(keep.tile([P, P], U8, name="h_plane%d_1" % m, align_bytes=64)[:])
-        late_stage = keep.tile([P, 2 * P * PACK], BF16, name="late_stage", align_bytes=64)
-        late_codes = keep.tile([P, 2 * P], U32, name="late_codes", tag="margin0", align_bytes=64)
-        late_plane = keep.tile([P, 2 * P], U8, name="late_plane", align_bytes=64)
-        for m in range(2):
-            grouped[m + 2][1] = late_stage[:, m * P * PACK : (m + 1) * P * PACK]
-            h_codes[m + 2].append(late_codes[:, m * P : (m + 1) * P])
-            h_plane[m + 2].append(late_plane[:, m * P : (m + 1) * P])
+        x_codes = [[keep.tile([P, HALF], U32, name="x_codes%d_%d" % (o, u), align_bytes=64) for u in range(2)] for o in range(PASSES)]
+        x_planes = keep.tile([P, S], U8, name="x_planes", tag="words0", align_bytes=64)
+        scores = [[psum.tile([P, HALF], F32, name="scores%d_%d" % (m, u)) for u in range(2)] for m in range(TILES)]
+        stage = [[keep.tile([P, PAIR * PACK], BF16, name="stage%d_%d" % (o, g), align_bytes=64) for g in range(2)] for o in range(PASSES)]
+        h_codes = [[keep.tile([P, PAIR], U32, name="h_codes%d_%d" % (o, g), align_bytes=64) for g in range(2)] for o in range(PASSES)]
+        h_plane = [[keep.tile([P, PAIR], U8, name="h_plane%d_%d" % (o, g), align_bytes=64) for g in range(2)] for o in range(PASSES)]
+        copied = [[keep.tile([P, HALF], F32, name="copied%d_%d" % (m, u), align_bytes=64) for u in range(2)] for m in range(TILES)]
+        gap = [keep.tile([P, S], F32, name="gap%d" % m, tag="gap%d" % (m % 3), align_bytes=64) for m in range(TILES)]
+        neg = [keep.tile([P, S], F32, name="neg%d" % m, tag="neg%d" % (m % 2), align_bytes=64) for m in range(TILES)]
         e = [keep.tile([P, S], F32, name="e%d" % m) for m in range(TILES)]
         prob = [keep.tile([P, S], F32, name="prob%d" % m) for m in range(TILES)]
+        total = [keep.tile([P, 1], F32, name="total%d" % m, tag="total%d" % m) for m in range(TILES)]
         low = [keep.tile([P, 1], F32, name="low%d" % m) for m in range(TILES)]
-        total = [keep.tile([P, 1], F32, name="total%d" % m) for m in range(TILES)]
         inv = [keep.tile([P, 1], F32, name="inv%d" % m) for m in range(TILES)]
 
-        def gather_words(o):
-            nc.vector.tensor_copy(x_codes[o][:], word_table[o][:].bitcast(U32).indirect(offsets[:]))
+        def cols(u):
+            return slice(u * HALF, (u + 1) * HALF)
 
-        def interleave(m, o):
-            raw = h_first[:, :, m * P : (m + 1) * P] if o == 0 else h_last[m // 2][:, :, (m % 2) * P : (m % 2 + 1) * P]
-            dst = grouped[m][o].rearrange("p (c i j) -> p c j i", i=PACK, j=PACK)
+        def gather_words(o, u):
+            part = offsets[:, u * HALF // LIST_ROWS : (u + 1) * HALF // LIST_ROWS]
+            nc.vector.tensor_copy(x_codes[o][u][:], word_table[o][:].bitcast(U32).indirect(part))
+
+        def interleave(o, g):
+            raw = h_raw[o][:, :, g * PAIR : (g + 1) * PAIR]
+            dst = stage[o][g][:].rearrange("p (c i j) -> p c j i", i=PACK, j=PACK)
             src = raw.rearrange("p j (c i) -> p c j i", i=PACK)
-            if (m, o) == (0, 1):
-                nc.vector.tensor_scalar(dst, src, SCALE, None, ALU.mult)
+            if g == 0:
+                nc.vector.tensor_copy(dst, src)
             else:
-                nc.scalar.activation(dst, src, ACT.Copy, scale=SCALE)
+                nc.scalar.activation(dst, src, ACT.Copy)
 
-        def quantize(m, o):
-            nc.vector.quantize_mx(
-                out=h_codes[m][o].bitcast(FP8X4),
-                scales=h_plane[m][o],
-                in_=grouped[m][o],
-            )
+        def quantize(o, g):
+            nc.vector.quantize_mx(out=h_codes[o][g][:].bitcast(FP8X4), scales=h_plane[o][g][:], in_=stage[o][g][:])
 
-        def multiply(m, o):
+        def multiply(m, o, u):
+            faces = slice((m % 2) * P, (m % 2 + 1) * P)
             nc.tensor.matmul_mx(
-                out=scores[m][:],
-                lhsT=h_codes[m][o].bitcast(FP8X4),
-                lhsT_scale=h_plane[m][o],
-                rhs=x_codes[o][:].bitcast(FP8X4),
-                rhs_scale=x_planes[PLANE_ROWS * o :, :],
+                out=scores[m][u][:],
+                lhsT=h_codes[o][m // 2][:, faces].bitcast(FP8X4),
+                lhsT_scale=h_plane[o][m // 2][:, faces],
+                rhs=x_codes[o][u][:].bitcast(FP8X4),
+                rhs_scale=x_planes[PLANE_ROWS * o :, cols(u)],
                 start=(o == 0),
                 stop=(o == PASSES - 1),
             )
 
-        def prepare(m, o):
-            interleave(m, o)
-            quantize(m, o)
-            multiply(m, o)
+        def subtract(m, u):
+            nc.vector.tensor_tensor(gap[m][:, cols(u)], margin[m][:, cols(u)], scores[m][u][:], ALU.subtract)
 
-        def subtract(m):
-            nc.vector.scalar_tensor_tensor(neg[m][:], margin[m][:], SCALE, scores[m][:], ALU.mult, ALU.subtract)
+        def subtract_aside(m, u):
+            nc.scalar.activation(copied[m][u][:], scores[m][u][:], ACT.Copy)
+            nc.gpsimd.tensor_tensor(gap[m][:, cols(u)], margin[m][:, cols(u)], copied[m][u][:], ALU.subtract)
 
         def lowest(m):
-            nc.vector.tensor_reduce(low[m][:], neg[m][:], mybir.AxisListType.X, ALU.min)
+            nc.vector.tensor_scalar(neg[m][:], gap[m][:], SCALE, None, ALU.mult, ALU.min, accum_out=low[m][:])
 
         def exponent(m):
             nc.scalar.activation(e[m][:], neg[m][:], ACT.Exp, bias=low[m][:], scale=-1.0, accum_out=total[m][:])
@@ -144,43 +126,53 @@ def tile_picked_zams_soft_p_kernel(tc, x_words, x_scales, hT, label, offs, out):
             nc.vector.reciprocal(inv[m][:], total[m][:])
 
         def finish(m):
-            if m == 0:
-                nc.scalar.activation(prob[m][:], e[m][:], ACT.Copy, scale=inv[m][:])
-            elif m == 1:
+            if m < 2:
                 nc.gpsimd.tensor_scalar(prob[m][:], e[m][:], inv[m][:], 0.0, ALU.mult, ALU.add)
             else:
                 nc.vector.tensor_scalar(prob[m][:], e[m][:], inv[m][:], None, ALU.mult)
             nc.sync.dma_start(out=out[m * P : (m + 1) * P, :], in_=prob[m][:])
 
-        for m in range(TILES):
-            interleave(m, 0)
+        for g in range(2):
+            interleave(0, g)
+        for g in range(2):
+            quantize(0, g)
+        for u in range(2):
+            gather_words(0, u)
         nc.vector.tensor_copy(x_planes[:], scale_table[:].indirect(offsets[:]))
+        for u in range(2):
+            for m in range(TILES):
+                multiply(m, 0, u)
+        for g in range(2):
+            interleave(1, g)
+        for g in range(2):
+            quantize(1, g)
+        gather_words(1, 0)
         for m in range(TILES):
-            quantize(m, 0)
-        gather_words(0)
+            multiply(m, 1, 0)
+        gather_words(1, 1)
         for m in range(TILES):
-            multiply(m, 0)
-        gather_words(1)
-        for m in range(AHEAD):
-            prepare(m, 1)
-        interleave(2, 1)
-        interleave(3, 1)
+            multiply(m, 1, 1)
 
-        subtract(0)
-        subtract(1)
-        nc.vector.quantize_mx(out=late_codes[:].bitcast(FP8X4), scales=late_plane[:], in_=late_stage[:])
-        multiply(2, 1)
-        multiply(3, 1)
-        for m in range(2):
-            lowest(m)
-            exponent(m)
-        for m in range(2):
-            subtract(m + 2)
-            invert(m)
-            finish(m)
-        for m in range(2, TILES):
-            lowest(m)
-            exponent(m)
+        subtract(0, 0)
+        subtract_aside(1, 0)
+        subtract(0, 1)
+        subtract_aside(2, 0)
+        subtract(1, 1)
+        subtract_aside(3, 0)
+        lowest(0)
+        exponent(0)
+        subtract(2, 1)
+        lowest(1)
+        exponent(1)
+        invert(0)
+        finish(0)
+        subtract(3, 1)
+        lowest(2)
+        exponent(2)
+        invert(1)
+        finish(1)
+        lowest(3)
+        exponent(3)
         for m in range(2, TILES):
             invert(m)
             finish(m)

@@ -31,6 +31,8 @@ def tile_picked_zams_soft_p_kernel(tc, x_words, x_scales, hT, label, offs, out):
     nc = tc.nc
     HALF = S // 2
     PAIR = 2 * P
+    WHOLE = slice(0, S)
+    HALVES = (slice(0, HALF), slice(HALF, S))
     with ExitStack() as ctx:
         keep = ctx.enter_context(tc.tile_pool(name="keep", bufs=1))
         psum = ctx.enter_context(tc.psum_pool(name="psum", bufs=1))
@@ -50,40 +52,45 @@ def tile_picked_zams_soft_p_kernel(tc, x_words, x_scales, hT, label, offs, out):
             rows = hT[o * K_PASS : (o + 1) * K_PASS, :]
             nc.sync.dma_start(out=h_raw[o][:], in_=rows.rearrange("(p j) c -> p j c", j=PACK))
 
+        def load_scales(r):
+            for o in range(PASSES):
+                nc.sync.dma_start(
+                    out=scale_table[PLANE_ROWS * o + r : P : QUADRANT, :].bitcast(I32),
+                    in_=x_scales[o, r :: PLANE_ROWS, :].bitcast(I32),
+                )
+
         load_h(0)
         nc.sync.dma_start(offsets[:], offs)
-        for q in range(QUADRANTS):
-            nc.sync.dma_start(
-                out=scale_table[QUADRANT * q : QUADRANT * q + PLANE_ROWS * PASSES, :].bitcast(I32),
-                in_=x_scales[:, PLANE_ROWS * q : PLANE_ROWS * (q + 1), :].bitcast(I32),
-            )
+        for r in range(PLANE_ROWS // 2):
+            load_scales(r)
         load_words(0)
+        for r in range(PLANE_ROWS // 2, PLANE_ROWS):
+            load_scales(r)
         load_h(1)
         load_words(1)
         for m in range(TILES):
             nc.sync.dma_start(out=margin[m][:], in_=label[m * P : (m + 1) * P, :])
 
-        x_codes = [[keep.tile([P, HALF], U32, name="x_codes%d_%d" % (o, u), align_bytes=64) for u in range(2)] for o in range(PASSES)]
+        pieces = [(m, c) for c in HALVES for m in (0, 1, 3)] + [(2, WHOLE)]
+        aside = [(1, HALVES[0]), (3, HALVES[0]), (3, HALVES[1])]
+        x_codes = [keep.tile([P, S], U32, name="x_codes%d" % o, align_bytes=64) for o in range(PASSES)]
         x_planes = keep.tile([P, S], U8, name="x_planes", tag="words0", align_bytes=64)
-        scores = [[psum.tile([P, HALF], F32, name="scores%d_%d" % (m, u)) for u in range(2)] for m in range(TILES)]
+        scores = {(m, c.start): psum.tile([P, c.stop - c.start], F32, name="scores%d_%d" % (m, c.start)) for m, c in pieces}
         stage = [[keep.tile([P, PAIR * PACK], BF16, name="stage%d_%d" % (o, g), align_bytes=64) for g in range(2)] for o in range(PASSES)]
         h_codes = [[keep.tile([P, PAIR], U32, name="h_codes%d_%d" % (o, g), align_bytes=64) for g in range(2)] for o in range(PASSES)]
         h_plane = [[keep.tile([P, PAIR], U8, name="h_plane%d_%d" % (o, g), align_bytes=64) for g in range(2)] for o in range(PASSES)]
-        copied = [[keep.tile([P, HALF], F32, name="copied%d_%d" % (m, u), align_bytes=64) for u in range(2)] for m in range(TILES)]
-        gap = [keep.tile([P, S], F32, name="gap%d" % m, tag="gap%d" % (m % 3), align_bytes=64) for m in range(TILES)]
+        copied = {(m, c.start): keep.tile([P, HALF], F32, name="copied%d_%d" % (m, c.start), tag="copied%d_%d" % (m, c.start), align_bytes=64) for m, c in aside}
+        gap = [keep.tile([P, S], F32, name="gap%d" % m, tag=("gap0", "gap1", "copied1_0", "gap3")[m], align_bytes=64) for m in range(TILES)]
         neg = [keep.tile([P, S], F32, name="neg%d" % m, tag="neg%d" % (m % 2), align_bytes=64) for m in range(TILES)]
         e = [keep.tile([P, S], F32, name="e%d" % m) for m in range(TILES)]
         prob = [keep.tile([P, S], F32, name="prob%d" % m) for m in range(TILES)]
-        total = [keep.tile([P, 1], F32, name="total%d" % m, tag="total%d" % m) for m in range(TILES)]
         low = [keep.tile([P, 1], F32, name="low%d" % m) for m in range(TILES)]
+        total = [keep.tile([P, 1], F32, name="total%d" % m) for m in range(TILES)]
         inv = [keep.tile([P, 1], F32, name="inv%d" % m) for m in range(TILES)]
 
-        def cols(u):
-            return slice(u * HALF, (u + 1) * HALF)
-
-        def gather_words(o, u):
-            part = offsets[:, u * HALF // LIST_ROWS : (u + 1) * HALF // LIST_ROWS]
-            nc.vector.tensor_copy(x_codes[o][u][:], word_table[o][:].bitcast(U32).indirect(part))
+        def gather_words(o, c):
+            part = offsets[:, c.start // LIST_ROWS : c.stop // LIST_ROWS]
+            nc.vector.tensor_copy(x_codes[o][:, c], word_table[o][:].bitcast(U32).indirect(part))
 
         def interleave(o, g):
             raw = h_raw[o][:, :, g * PAIR : (g + 1) * PAIR]
@@ -97,24 +104,24 @@ def tile_picked_zams_soft_p_kernel(tc, x_words, x_scales, hT, label, offs, out):
         def quantize(o, g):
             nc.vector.quantize_mx(out=h_codes[o][g][:].bitcast(FP8X4), scales=h_plane[o][g][:], in_=stage[o][g][:])
 
-        def multiply(m, o, u):
+        def multiply(m, c, o):
             faces = slice((m % 2) * P, (m % 2 + 1) * P)
             nc.tensor.matmul_mx(
-                out=scores[m][u][:],
+                out=scores[m, c.start][:],
                 lhsT=h_codes[o][m // 2][:, faces].bitcast(FP8X4),
                 lhsT_scale=h_plane[o][m // 2][:, faces],
-                rhs=x_codes[o][u][:].bitcast(FP8X4),
-                rhs_scale=x_planes[PLANE_ROWS * o :, cols(u)],
+                rhs=x_codes[o][:, c].bitcast(FP8X4),
+                rhs_scale=x_planes[PLANE_ROWS * o :, c],
                 start=(o == 0),
                 stop=(o == PASSES - 1),
             )
 
-        def subtract(m, u):
-            nc.vector.tensor_tensor(gap[m][:, cols(u)], margin[m][:, cols(u)], scores[m][u][:], ALU.subtract)
+        def subtract(m, c):
+            nc.vector.tensor_tensor(gap[m][:, c], margin[m][:, c], scores[m, c.start][:], ALU.subtract)
 
-        def subtract_aside(m, u):
-            nc.scalar.activation(copied[m][u][:], scores[m][u][:], ACT.Copy)
-            nc.gpsimd.tensor_tensor(gap[m][:, cols(u)], margin[m][:, cols(u)], copied[m][u][:], ALU.subtract)
+        def subtract_aside(m, c):
+            nc.scalar.activation(copied[m, c.start][:], scores[m, c.start][:], ACT.Copy)
+            nc.gpsimd.tensor_tensor(gap[m][:, c], margin[m][:, c], copied[m, c.start][:], ALU.subtract)
 
         def lowest(m):
             nc.vector.tensor_scalar(neg[m][:], gap[m][:], SCALE, None, ALU.mult, ALU.min, accum_out=low[m][:])
@@ -126,53 +133,46 @@ def tile_picked_zams_soft_p_kernel(tc, x_words, x_scales, hT, label, offs, out):
             nc.vector.reciprocal(inv[m][:], total[m][:])
 
         def finish(m):
-            if m < 2:
-                nc.gpsimd.tensor_scalar(prob[m][:], e[m][:], inv[m][:], 0.0, ALU.mult, ALU.add)
-            else:
-                nc.vector.tensor_scalar(prob[m][:], e[m][:], inv[m][:], None, ALU.mult)
-            nc.sync.dma_start(out=out[m * P : (m + 1) * P, :], in_=prob[m][:])
+            for c in HALVES if m == TILES - 1 else (WHOLE,):
+                if m < 2:
+                    nc.gpsimd.tensor_scalar(prob[m][:, c], e[m][:, c], inv[m][:], 0.0, ALU.mult, ALU.add)
+                else:
+                    nc.vector.tensor_scalar(prob[m][:, c], e[m][:, c], inv[m][:], None, ALU.mult)
+                nc.sync.dma_start(out=out[m * P : (m + 1) * P, c], in_=prob[m][:, c])
 
         for g in range(2):
             interleave(0, g)
         for g in range(2):
             quantize(0, g)
-        for u in range(2):
-            gather_words(0, u)
+        gather_words(0, WHOLE)
         nc.vector.tensor_copy(x_planes[:], scale_table[:].indirect(offsets[:]))
-        for u in range(2):
-            for m in range(TILES):
-                multiply(m, 0, u)
+        for m, c in pieces:
+            multiply(m, c, 0)
         for g in range(2):
             interleave(1, g)
         for g in range(2):
             quantize(1, g)
-        gather_words(1, 0)
-        for m in range(TILES):
-            multiply(m, 1, 0)
-        gather_words(1, 1)
-        for m in range(TILES):
-            multiply(m, 1, 1)
+        for c in HALVES:
+            gather_words(1, c)
+        for m, c in pieces:
+            multiply(m, c, 1)
 
-        subtract(0, 0)
-        subtract_aside(1, 0)
-        subtract(0, 1)
-        subtract_aside(2, 0)
-        subtract(1, 1)
-        subtract_aside(3, 0)
+        subtract(0, HALVES[0])
+        subtract_aside(1, HALVES[0])
+        subtract_aside(3, HALVES[0])
+        subtract(0, HALVES[1])
+        subtract(1, HALVES[1])
+        subtract_aside(3, HALVES[1])
         lowest(0)
         exponent(0)
-        subtract(2, 1)
         lowest(1)
         exponent(1)
-        invert(0)
-        finish(0)
-        subtract(3, 1)
-        lowest(2)
-        exponent(2)
-        invert(1)
-        finish(1)
-        lowest(3)
-        exponent(3)
+        subtract(2, WHOLE)
+        for m in range(2):
+            invert(m)
+            finish(m)
+            lowest(m + 2)
+            exponent(m + 2)
         for m in range(2, TILES):
             invert(m)
             finish(m)

@@ -71,8 +71,8 @@ def tile_picked_zams_soft_p_kernel(tc, x_words, x_scales, hT, label, offs, out):
         for m in range(TILES):
             nc.sync.dma_start(out=margin[m][:], in_=label[m * P : (m + 1) * P, :])
 
-        pieces = [(m, c) for c in HALVES for m in (0, 1, 3)] + [(2, WHOLE)]
-        aside = [(1, HALVES[0]), (3, HALVES[0]), (3, HALVES[1])]
+        pieces = [(m, c) for c in HALVES for m in range(TILES)]
+        aside = [(2, HALVES[0]), (2, HALVES[1]), (3, HALVES[0])]
         x_codes = [keep.tile([P, S], U32, name="x_codes%d" % o, align_bytes=64) for o in range(PASSES)]
         x_planes = keep.tile([P, S], U8, name="x_planes", tag="words0", align_bytes=64)
         scores = {(m, c.start): psum.tile([P, c.stop - c.start], F32, name="scores%d_%d" % (m, c.start)) for m, c in pieces}
@@ -80,7 +80,7 @@ def tile_picked_zams_soft_p_kernel(tc, x_words, x_scales, hT, label, offs, out):
         h_codes = [[keep.tile([P, PAIR], U32, name="h_codes%d_%d" % (o, g), align_bytes=64) for g in range(2)] for o in range(PASSES)]
         h_plane = [[keep.tile([P, PAIR], U8, name="h_plane%d_%d" % (o, g), align_bytes=64) for g in range(2)] for o in range(PASSES)]
         copied = {(m, c.start): keep.tile([P, HALF], F32, name="copied%d_%d" % (m, c.start), tag="copied%d_%d" % (m, c.start), align_bytes=64) for m, c in aside}
-        gap = [keep.tile([P, S], F32, name="gap%d" % m, tag=("gap0", "gap1", "copied1_0", "gap3")[m], align_bytes=64) for m in range(TILES)]
+        gap = [keep.tile([P, S], F32, name="gap%d" % m, tag="gap%d" % (m % 3), align_bytes=64) for m in range(TILES)]
         neg = [keep.tile([P, S], F32, name="neg%d" % m, tag="neg%d" % (m % 2), align_bytes=64) for m in range(TILES)]
         e = [keep.tile([P, S], F32, name="e%d" % m) for m in range(TILES)]
         prob = [keep.tile([P, S], F32, name="prob%d" % m) for m in range(TILES)]
@@ -132,13 +132,14 @@ def tile_picked_zams_soft_p_kernel(tc, x_words, x_scales, hT, label, offs, out):
         def invert(m):
             nc.vector.reciprocal(inv[m][:], total[m][:])
 
-        def finish(m):
-            for c in HALVES if m == TILES - 1 else (WHOLE,):
-                if m < 2:
-                    nc.gpsimd.tensor_scalar(prob[m][:, c], e[m][:, c], inv[m][:], 0.0, ALU.mult, ALU.add)
-                else:
-                    nc.vector.tensor_scalar(prob[m][:, c], e[m][:, c], inv[m][:], None, ALU.mult)
-                nc.sync.dma_start(out=out[m * P : (m + 1) * P, c], in_=prob[m][:, c])
+        def normalise(m, c):
+            nc.vector.tensor_scalar(prob[m][:, c], e[m][:, c], inv[m][:], None, ALU.mult)
+
+        def normalise_aside(m, c):
+            nc.gpsimd.tensor_scalar(prob[m][:, c], e[m][:, c], inv[m][:], 0.0, ALU.mult, ALU.add)
+
+        def store(m, c):
+            nc.sync.dma_start(out=out[m * P : (m + 1) * P, c], in_=prob[m][:, c])
 
         for g in range(2):
             interleave(0, g)
@@ -157,22 +158,31 @@ def tile_picked_zams_soft_p_kernel(tc, x_words, x_scales, hT, label, offs, out):
         for m, c in pieces:
             multiply(m, c, 1)
 
-        subtract(0, HALVES[0])
-        subtract_aside(1, HALVES[0])
-        subtract_aside(3, HALVES[0])
-        subtract(0, HALVES[1])
-        subtract(1, HALVES[1])
-        subtract_aside(3, HALVES[1])
-        lowest(0)
-        exponent(0)
-        lowest(1)
-        exponent(1)
-        subtract(2, WHOLE)
+        for c in HALVES:
+            for m in range(2):
+                subtract(m, c)
+        for m, c in aside:
+            subtract_aside(m, c)
         for m in range(2):
-            invert(m)
-            finish(m)
-            lowest(m + 2)
-            exponent(m + 2)
-        for m in range(2, TILES):
-            invert(m)
-            finish(m)
+            lowest(m)
+            exponent(m)
+        subtract(3, HALVES[1])
+        invert(0)
+        normalise_aside(0, HALVES[0])
+        nc.scalar.activation(prob[0][:, HALVES[1]], e[0][:, HALVES[1]], ACT.Copy, scale=inv[0][:])
+        store(0, WHOLE)
+        lowest(2)
+        exponent(2)
+        invert(1)
+        normalise_aside(1, HALVES[0])
+        lowest(3)
+        exponent(3)
+        invert(2)
+        normalise(1, HALVES[1])
+        store(1, WHOLE)
+        normalise(2, WHOLE)
+        store(2, WHOLE)
+        invert(3)
+        for c in HALVES:
+            normalise(3, c)
+            store(3, c)

@@ -71,7 +71,7 @@ def tile_picked_zams_soft_p_kernel(tc, x_words, x_scales, hT, label, offs, out):
         for m in range(TILES):
             nc.sync.dma_start(out=margin[m][:], in_=label[m * P : (m + 1) * P, :])
 
-        pieces = [(m, c) for c in HALVES for m in range(TILES)]
+        pieces = [(m, c) for c in HALVES for m in (0, 2, 1)] + [(3, WHOLE)]
         aside = [(2, HALVES[0]), (2, HALVES[1]), (3, HALVES[0])]
         x_codes = [keep.tile([P, S], U32, name="x_codes%d" % o, align_bytes=64) for o in range(PASSES)]
         x_planes = keep.tile([P, S], U8, name="x_planes", tag="words0", align_bytes=64)
@@ -116,11 +116,14 @@ def tile_picked_zams_soft_p_kernel(tc, x_words, x_scales, hT, label, offs, out):
                 stop=(o == PASSES - 1),
             )
 
+        def score(m, c):
+            return scores[m, 0][:, c] if m == TILES - 1 else scores[m, c.start][:]
+
         def subtract(m, c):
-            nc.vector.tensor_tensor(gap[m][:, c], margin[m][:, c], scores[m, c.start][:], ALU.subtract)
+            nc.vector.tensor_tensor(gap[m][:, c], margin[m][:, c], score(m, c), ALU.subtract)
 
         def subtract_aside(m, c):
-            nc.scalar.activation(copied[m, c.start][:], scores[m, c.start][:], ACT.Copy)
+            nc.scalar.activation(copied[m, c.start][:], score(m, c), ACT.Copy)
             nc.gpsimd.tensor_tensor(gap[m][:, c], margin[m][:, c], copied[m, c.start][:], ALU.subtract)
 
         def lowest(m):

@@ -41,9 +41,13 @@ def tile_picked_zams_soft_p_kernel(tc, x_words, x_scales, hT, label, offs, out):
         scale_table = keep.tile([P, T], U8, name="scale_table", align_bytes=64)
         word_table = [keep.tile([P, T], I32, name="word_table%d" % o, tag="words%d" % o, align_bytes=64) for o in range(PASSES)]
         h_raw = [keep.tile([P, PACK, J], F32, name="h_raw%d" % o, align_bytes=64) for o in range(PASSES)]
-        margin = [keep.tile([P, S], F32, name="margin%d" % m, align_bytes=64) for m in range(TILES)]
+        picked = keep.tile([P, S], U8, name="picked", tag="late", align_bytes=64)
+        margin0 = keep.tile([P, S], F32, name="margin0", align_bytes=64)
+        x_planes = keep.tile([P, PASSES * S], U8, name="x_planes", align_bytes=64)
 
-        nc.vector.memset(scale_table[:].bitcast(I32), 0)
+        nc.vector.memset(scale_table[QUADRANT : 2 * QUADRANT, :].bitcast(I32), 0)
+        nc.vector.memset(scale_table[2 * QUADRANT :, :].bitcast(I32), 0)
+        nc.vector.memset(x_planes[:].bitcast(I32), 0)
 
         def load_words(o):
             nc.sync.dma_start(out=word_table[o][:], in_=x_words[o].rearrange("p n t -> p (n t)").bitcast(I32))
@@ -52,29 +56,29 @@ def tile_picked_zams_soft_p_kernel(tc, x_words, x_scales, hT, label, offs, out):
             rows = hT[o * K_PASS : (o + 1) * K_PASS, :]
             nc.sync.dma_start(out=h_raw[o][:], in_=rows.rearrange("(p j) c -> p j c", j=PACK))
 
-        def load_scales(r):
-            for o in range(PASSES):
-                nc.sync.dma_start(
-                    out=scale_table[PLANE_ROWS * o + r : P : QUADRANT, :].bitcast(I32),
-                    in_=x_scales[o, r :: PLANE_ROWS, :].bitcast(I32),
-                )
-
         load_h(0)
         nc.sync.dma_start(offsets[:], offs)
-        for r in range(PLANE_ROWS // 2):
-            load_scales(r)
+        for o in range(PASSES):
+            nc.sync.dma_start(out=scale_table[o:QUADRANT:PASSES, :].bitcast(I32), in_=x_scales[o].bitcast(I32))
         load_words(0)
-        for r in range(PLANE_ROWS // 2, PLANE_ROWS):
-            load_scales(r)
         load_h(1)
         load_words(1)
-        for m in range(TILES):
-            nc.sync.dma_start(out=margin[m][:], in_=label[m * P : (m + 1) * P, :])
+        nc.sync.dma_start(out=margin0[:], in_=label[0:P, :])
+        nc.vector.tensor_copy(picked[:], scale_table[:].indirect(offsets[:]))
+        rows = PASSES * PLANE_ROWS
+        for q in range(QUADRANTS):
+            nc.scalar.dma_start(
+                out=x_planes[QUADRANT * q : QUADRANT * q + PLANE_ROWS, :].bitcast(I32),
+                in_=picked[rows * q : rows * (q + 1), :].bitcast(I32),
+            )
+        margins = keep.tile([P, TILES - 1, S], F32, name="margins", tag="late", align_bytes=64)
+        margin = [margin0[:]] + [margins[:, m, :] for m in range(TILES - 1)]
+        for m in range(1, TILES):
+            nc.sync.dma_start(out=margin[m], in_=label[m * P : (m + 1) * P, :])
 
         pieces = [(m, c) for c in HALVES for m in (0, 2, 1)] + [(3, WHOLE)]
         aside = [(2, HALVES[0]), (2, HALVES[1]), (3, HALVES[0])]
         x_codes = [keep.tile([P, S], U32, name="x_codes%d" % o, align_bytes=64) for o in range(PASSES)]
-        x_planes = keep.tile([P, S], U8, name="x_planes", tag="words0", align_bytes=64)
         scores = {(m, c.start): psum.tile([P, c.stop - c.start], F32, name="scores%d_%d" % (m, c.start)) for m, c in pieces}
         stage = [[keep.tile([P, PAIR * PACK], BF16, name="stage%d_%d" % (o, g), align_bytes=64) for g in range(2)] for o in range(PASSES)]
         h_codes = [[keep.tile([P, PAIR], U32, name="h_codes%d_%d" % (o, g), align_bytes=64) for g in range(2)] for o in range(PASSES)]
@@ -111,7 +115,7 @@ def tile_picked_zams_soft_p_kernel(tc, x_words, x_scales, hT, label, offs, out):
                 lhsT=h_codes[o][m // 2][:, faces].bitcast(FP8X4),
                 lhsT_scale=h_plane[o][m // 2][:, faces],
                 rhs=x_codes[o][:, c].bitcast(FP8X4),
-                rhs_scale=x_planes[PLANE_ROWS * o :, c],
+                rhs_scale=x_planes[:, o * S + c.start : o * S + c.stop],
                 start=(o == 0),
                 stop=(o == PASSES - 1),
             )
@@ -149,7 +153,6 @@ def tile_picked_zams_soft_p_kernel(tc, x_words, x_scales, hT, label, offs, out):
         for g in range(2):
             quantize(0, g)
         gather_words(0, WHOLE)
-        nc.vector.tensor_copy(x_planes[:], scale_table[:].indirect(offsets[:]))
         for m, c in pieces:
             multiply(m, c, 0)
         for g in range(2):

@@ -38,11 +38,10 @@ def tile_picked_zams_soft_p_kernel(tc, x_words, x_scales, hT, label, offs, out):
         psum = ctx.enter_context(tc.psum_pool(name="psum", bufs=1))
 
         offsets = keep.tile([P, S // LIST_ROWS], U16, name="offsets")
-        scale_table = keep.tile([P, T], U8, name="scale_table", align_bytes=64)
+        scale_table = keep.tile([P, T], U8, name="scale_table", tag="words1", align_bytes=64)
         word_table = [keep.tile([P, T], I32, name="word_table%d" % o, tag="words%d" % o, align_bytes=64) for o in range(PASSES)]
-        h_raw = [keep.tile([P, PACK, J], F32, name="h_raw%d" % o, align_bytes=64) for o in range(PASSES)]
-        picked = keep.tile([P, S], U8, name="picked", tag="late", align_bytes=64)
-        margin0 = keep.tile([P, S], F32, name="margin0", align_bytes=64)
+        h_raw = [keep.tile([P, PACK, J], F32, name="h_raw%d" % o, tag="raw%d" % o, align_bytes=64) for o in range(PASSES)]
+        picked = keep.tile([P, S], U8, name="picked", align_bytes=64)
         x_planes = keep.tile([P, PASSES * S], U8, name="x_planes", align_bytes=64)
 
         nc.vector.memset(scale_table[QUADRANT : 2 * QUADRANT, :].bitcast(I32), 0)
@@ -60,21 +59,16 @@ def tile_picked_zams_soft_p_kernel(tc, x_words, x_scales, hT, label, offs, out):
         nc.sync.dma_start(offsets[:], offs)
         for o in range(PASSES):
             nc.sync.dma_start(out=scale_table[o:QUADRANT:PASSES, :].bitcast(I32), in_=x_scales[o].bitcast(I32))
-        load_words(0)
         load_h(1)
-        load_words(1)
-        nc.sync.dma_start(out=margin0[:], in_=label[0:P, :])
+        load_words(0)
         nc.vector.tensor_copy(picked[:], scale_table[:].indirect(offsets[:]))
         rows = PASSES * PLANE_ROWS
         for q in range(QUADRANTS):
-            nc.scalar.dma_start(
+            nc.sync.dma_start(
                 out=x_planes[QUADRANT * q : QUADRANT * q + PLANE_ROWS, :].bitcast(I32),
                 in_=picked[rows * q : rows * (q + 1), :].bitcast(I32),
             )
-        margins = keep.tile([P, TILES - 1, S], F32, name="margins", tag="late", align_bytes=64)
-        margin = [margin0[:]] + [margins[:, m, :] for m in range(TILES - 1)]
-        for m in range(1, TILES):
-            nc.sync.dma_start(out=margin[m], in_=label[m * P : (m + 1) * P, :])
+        load_words(1)
 
         pieces = [(m, c) for c in HALVES for m in (0, 2, 1)] + [(3, WHOLE)]
         aside = [(2, HALVES[0]), (2, HALVES[1]), (3, HALVES[0])]
@@ -150,15 +144,20 @@ def tile_picked_zams_soft_p_kernel(tc, x_words, x_scales, hT, label, offs, out):
 
         for g in range(2):
             interleave(0, g)
+        margins = keep.tile([P, TILES, S], F32, name="margins", tag="raw0", align_bytes=64)
+        margin = [margins[:, m, :] for m in range(TILES)]
+        for m in range(TILES):
+            nc.sync.dma_start(out=margin[m], in_=label[m * P : (m + 1) * P, :])
         for g in range(2):
             quantize(0, g)
-        gather_words(0, WHOLE)
-        for m, c in pieces:
-            multiply(m, c, 0)
         for g in range(2):
             interleave(1, g)
         for g in range(2):
             quantize(1, g)
+        for c in HALVES:
+            gather_words(0, c)
+        for m, c in pieces:
+            multiply(m, c, 0)
         for c in HALVES:
             gather_words(1, c)
         for m, c in pieces:

@@ -48,19 +48,20 @@ def tile_picked_zams_soft_p_kernel(tc, x_words, x_scales, hT, label, offs, out):
         nc.vector.memset(scale_table[2 * QUADRANT :, :].bitcast(I32), 0)
         nc.vector.memset(x_planes[:].bitcast(I32), 0)
 
-        def load_words(o):
-            nc.sync.dma_start(out=word_table[o][:], in_=x_words[o].rearrange("p n t -> p (n t)").bitcast(I32))
+        def load_words(o, c):
+            nc.sync.dma_start(out=word_table[o][:, c], in_=x_words[o].rearrange("p n t -> p (n t)").bitcast(I32)[:, c])
 
         def load_h(o):
             rows = hT[o * K_PASS : (o + 1) * K_PASS, :]
             nc.sync.dma_start(out=h_raw[o][:], in_=rows.rearrange("(p j) c -> p j c", j=PACK))
 
-        load_h(0)
+        load_words(0, slice(0, T // 2))
         nc.sync.dma_start(offsets[:], offs)
         for o in range(PASSES):
             nc.sync.dma_start(out=scale_table[o:QUADRANT:PASSES, :].bitcast(I32), in_=x_scales[o].bitcast(I32))
+        load_words(0, slice(T // 2, T))
+        load_h(0)
         load_h(1)
-        load_words(0)
         nc.vector.tensor_copy(picked[:], scale_table[:].indirect(offsets[:]))
         rows = PASSES * PLANE_ROWS
         for q in range(QUADRANTS):
@@ -68,7 +69,7 @@ def tile_picked_zams_soft_p_kernel(tc, x_words, x_scales, hT, label, offs, out):
                 out=x_planes[QUADRANT * q : QUADRANT * q + PLANE_ROWS, :].bitcast(I32),
                 in_=picked[rows * q : rows * (q + 1), :].bitcast(I32),
             )
-        load_words(1)
+        load_words(1, slice(0, T))
 
         pieces = [(m, c) for c in HALVES for m in (0, 2, 1)] + [(3, WHOLE)]
         aside = [(2, HALVES[0]), (2, HALVES[1]), (3, HALVES[0])]
@@ -142,6 +143,7 @@ def tile_picked_zams_soft_p_kernel(tc, x_words, x_scales, hT, label, offs, out):
         def store(m, c):
             nc.sync.dma_start(out=out[m * P : (m + 1) * P, c], in_=prob[m][:, c])
 
+        gather_words(0, WHOLE)
         for g in range(2):
             interleave(0, g)
         margins = keep.tile([P, TILES, S], F32, name="margins", tag="raw0", align_bytes=64)
@@ -154,8 +156,6 @@ def tile_picked_zams_soft_p_kernel(tc, x_words, x_scales, hT, label, offs, out):
             interleave(1, g)
         for g in range(2):
             quantize(1, g)
-        for c in HALVES:
-            gather_words(0, c)
         for m, c in pieces:
             multiply(m, c, 0)
         for c in HALVES:

@@ -29,6 +29,7 @@ ACT = mybir.ActivationFunctionType
 
 def tile_picked_zams_soft_p_kernel(tc, x_words, x_scales, hT, label, offs, out):
     nc = tc.nc
+    SPREAD = 4
     HALF = S // 2
     PAIR = 2 * P
     WHOLE = slice(0, S)
@@ -44,8 +45,7 @@ def tile_picked_zams_soft_p_kernel(tc, x_words, x_scales, hT, label, offs, out):
         picked = keep.tile([P, S], U8, name="picked", align_bytes=64)
         x_planes = keep.tile([P, PASSES * S], U8, name="x_planes", align_bytes=64)
 
-        nc.vector.memset(scale_table[QUADRANT : 2 * QUADRANT, :].bitcast(I32), 0)
-        nc.vector.memset(scale_table[2 * QUADRANT :, :].bitcast(I32), 0)
+        nc.vector.memset(scale_table[:].bitcast(I32), 0)
         nc.vector.memset(x_planes[:].bitcast(I32), 0)
 
         def load_words(o, c):
@@ -58,16 +58,15 @@ def tile_picked_zams_soft_p_kernel(tc, x_words, x_scales, hT, label, offs, out):
         load_words(0, slice(0, T // 2))
         nc.sync.dma_start(offsets[:], offs)
         for o in range(PASSES):
-            nc.sync.dma_start(out=scale_table[o:QUADRANT:PASSES, :].bitcast(I32), in_=x_scales[o].bitcast(I32))
+            nc.sync.dma_start(out=scale_table[SPREAD * o :: SPREAD * PASSES, :].bitcast(I32), in_=x_scales[o].bitcast(I32))
         load_words(0, slice(T // 2, T))
         load_h(0)
         load_h(1)
         nc.vector.tensor_copy(picked[:], scale_table[:].indirect(offsets[:]))
-        rows = PASSES * PLANE_ROWS
         for q in range(QUADRANTS):
             nc.sync.dma_start(
                 out=x_planes[QUADRANT * q : QUADRANT * q + PLANE_ROWS, :].bitcast(I32),
-                in_=picked[rows * q : rows * (q + 1), :].bitcast(I32),
+                in_=picked[QUADRANT * q : QUADRANT * (q + 1) : SPREAD, :].bitcast(I32),
             )
         load_words(1, slice(0, T))
 
@@ -79,8 +78,8 @@ def tile_picked_zams_soft_p_kernel(tc, x_words, x_scales, hT, label, offs, out):
         h_codes = [[keep.tile([P, PAIR], U32, name="h_codes%d_%d" % (o, g), align_bytes=64) for g in range(2)] for o in range(PASSES)]
         h_plane = [[keep.tile([P, PAIR], U8, name="h_plane%d_%d" % (o, g), align_bytes=64) for g in range(2)] for o in range(PASSES)]
         copied = {(m, c.start): keep.tile([P, HALF], F32, name="copied%d_%d" % (m, c.start), tag="copied%d_%d" % (m, c.start), align_bytes=64) for m, c in aside}
-        gap = [keep.tile([P, S], F32, name="gap%d" % m, tag="gap%d" % (m % 3), align_bytes=64) for m in range(TILES)]
-        neg = [keep.tile([P, S], F32, name="neg%d" % m, tag="neg%d" % (m % 2), align_bytes=64) for m in range(TILES)]
+        gap = [keep.tile([P, S], F32, name="gap%d" % m, tag="gap%d" % m, align_bytes=64) for m in range(TILES)]
+        neg = gap[:2] + [keep.tile([P, S], F32, name="neg%d" % m, tag="gap%d" % (m % 2), align_bytes=64) for m in range(2, TILES)]
         e = [keep.tile([P, S], F32, name="e%d" % m) for m in range(TILES)]
         prob = [keep.tile([P, S], F32, name="prob%d" % m) for m in range(TILES)]
         low = [keep.tile([P, 1], F32, name="low%d" % m) for m in range(TILES)]
@@ -96,9 +95,9 @@ def tile_picked_zams_soft_p_kernel(tc, x_words, x_scales, hT, label, offs, out):
             dst = stage[o][g][:].rearrange("p (c i j) -> p c j i", i=PACK, j=PACK)
             src = raw.rearrange("p j (c i) -> p c j i", i=PACK)
             if g == 0:
-                nc.vector.tensor_copy(dst, src)
+                nc.vector.tensor_scalar(dst, src, SCALE, None, ALU.mult)
             else:
-                nc.scalar.activation(dst, src, ACT.Copy)
+                nc.scalar.activation(dst, src, ACT.Copy, scale=SCALE)
 
         def quantize(o, g):
             nc.vector.quantize_mx(out=h_codes[o][g][:].bitcast(FP8X4), scales=h_plane[o][g][:], in_=stage[o][g][:])
@@ -119,14 +118,20 @@ def tile_picked_zams_soft_p_kernel(tc, x_words, x_scales, hT, label, offs, out):
             return scores[m, 0][:, c] if m == TILES - 1 else scores[m, c.start][:]
 
         def subtract(m, c):
-            nc.vector.tensor_tensor(gap[m][:, c], margin[m][:, c], score(m, c), ALU.subtract)
+            if m < 2:
+                nc.vector.scalar_tensor_tensor(gap[m][:, c], margin[m][:, c], SCALE, score(m, c), ALU.mult, ALU.subtract)
+            else:
+                nc.vector.scalar_tensor_tensor(gap[m][:, c], score(m, c), -1.0 / SCALE, margin[m][:, c], ALU.mult, ALU.add)
 
         def subtract_aside(m, c):
-            nc.scalar.activation(copied[m, c.start][:], score(m, c), ACT.Copy)
+            nc.scalar.activation(copied[m, c.start][:], score(m, c), ACT.Copy, scale=1.0 / SCALE)
             nc.gpsimd.tensor_tensor(gap[m][:, c], margin[m][:, c], copied[m, c.start][:], ALU.subtract)
 
         def lowest(m):
-            nc.vector.tensor_scalar(neg[m][:], gap[m][:], SCALE, None, ALU.mult, ALU.min, accum_out=low[m][:])
+            if m < 2:
+                nc.vector.tensor_reduce(low[m][:], gap[m][:], mybir.AxisListType.X, ALU.min)
+            else:
+                nc.vector.tensor_scalar(neg[m][:], gap[m][:], SCALE, None, ALU.mult, ALU.min, accum_out=low[m][:])
 
         def exponent(m):
             nc.scalar.activation(e[m][:], neg[m][:], ACT.Exp, bias=low[m][:], scale=-1.0, accum_out=total[m][:])

@@ -8,13 +8,18 @@ PACK = 4
 K_PASS = P * PACK
 PASSES = K // K_PASS
 TILES = J // P
+PAIR = 2 * P
+PAIRS = J // PAIR
 QUADRANTS = 4
 QUADRANT = P // QUADRANTS
 PLANE_ROWS = 4
+SPREAD = QUADRANT // (PASSES * PLANE_ROWS)
 LIST_ROWS = 16
 SCALE = 4.0
-AHEAD = 2
 FLOPS = 2 * K * J * S
+
+WHOLE = slice(0, S)
+FRONT, BACK = slice(0, S // 2), slice(S // 2, S)
 
 F32 = mybir.dt.float32
 BF16 = mybir.dt.bfloat16
@@ -29,11 +34,6 @@ ACT = mybir.ActivationFunctionType
 
 def tile_picked_zams_soft_p_kernel(tc, x_words, x_scales, hT, label, offs, out):
     nc = tc.nc
-    SPREAD = 4
-    HALF = S // 2
-    PAIR = 2 * P
-    WHOLE = slice(0, S)
-    HALVES = (slice(0, HALF), slice(HALF, S))
     with ExitStack() as ctx:
         keep = ctx.enter_context(tc.tile_pool(name="keep", bufs=1))
         psum = ctx.enter_context(tc.psum_pool(name="psum", bufs=1))
@@ -42,45 +42,47 @@ def tile_picked_zams_soft_p_kernel(tc, x_words, x_scales, hT, label, offs, out):
         scale_table = keep.tile([P, T], U8, name="scale_table", tag="words1", align_bytes=64)
         word_table = [keep.tile([P, T], I32, name="word_table%d" % o, tag="words%d" % o, align_bytes=64) for o in range(PASSES)]
         h_raw = [keep.tile([P, PACK, J], F32, name="h_raw%d" % o, tag="raw%d" % o, align_bytes=64) for o in range(PASSES)]
-        picked = keep.tile([P, S], U8, name="picked", align_bytes=64)
+        x_scales_picked = keep.tile([P, S], U8, name="x_scales_picked", align_bytes=64)
         x_planes = keep.tile([P, PASSES * S], U8, name="x_planes", align_bytes=64)
 
         nc.vector.memset(scale_table[:].bitcast(I32), 0)
         nc.vector.memset(x_planes[:].bitcast(I32), 0)
 
-        def load_words(o, c):
-            nc.sync.dma_start(out=word_table[o][:, c], in_=x_words[o].rearrange("p n t -> p (n t)").bitcast(I32)[:, c])
+        def load_words(o, columns):
+            words = x_words[o].rearrange("p n t -> p (n t)").bitcast(I32)
+            nc.sync.dma_start(out=word_table[o][:, columns], in_=words[:, columns])
 
         def load_h(o):
             rows = hT[o * K_PASS : (o + 1) * K_PASS, :]
-            nc.sync.dma_start(out=h_raw[o][:], in_=rows.rearrange("(p j) c -> p j c", j=PACK))
+            nc.sync.dma_start(out=h_raw[o][:], in_=rows.rearrange("(p r) c -> p r c", r=PACK))
 
         load_words(0, slice(0, T // 2))
         nc.sync.dma_start(offsets[:], offs)
         for o in range(PASSES):
             nc.sync.dma_start(out=scale_table[SPREAD * o :: SPREAD * PASSES, :].bitcast(I32), in_=x_scales[o].bitcast(I32))
         load_words(0, slice(T // 2, T))
-        load_h(0)
-        load_h(1)
-        nc.vector.tensor_copy(picked[:], scale_table[:].indirect(offsets[:]))
+        for o in range(PASSES):
+            load_h(o)
+        nc.vector.tensor_copy(x_scales_picked[:], scale_table[:].indirect(offsets[:]))
         for q in range(QUADRANTS):
+            first = QUADRANT * q
             nc.sync.dma_start(
-                out=x_planes[QUADRANT * q : QUADRANT * q + PLANE_ROWS, :].bitcast(I32),
-                in_=picked[QUADRANT * q : QUADRANT * (q + 1) : SPREAD, :].bitcast(I32),
+                out=x_planes[first : first + PLANE_ROWS, :].bitcast(I32),
+                in_=x_scales_picked[first : first + QUADRANT : SPREAD, :].bitcast(I32),
             )
         load_words(1, slice(0, T))
 
-        pieces = [(m, c) for c in HALVES for m in (0, 2, 1)] + [(3, WHOLE)]
-        aside = [(2, HALVES[0]), (2, HALVES[1]), (3, HALVES[0])]
+        pieces = [(m, c) for c in (FRONT, BACK) for m in (0, 2, 1)] + [(3, WHOLE)]
+        aside = [(2, FRONT), (2, BACK), (3, FRONT)]
         x_codes = [keep.tile([P, S], U32, name="x_codes%d" % o, align_bytes=64) for o in range(PASSES)]
         scores = {(m, c.start): psum.tile([P, c.stop - c.start], F32, name="scores%d_%d" % (m, c.start)) for m, c in pieces}
-        stage = [[keep.tile([P, PAIR * PACK], BF16, name="stage%d_%d" % (o, g), align_bytes=64) for g in range(2)] for o in range(PASSES)]
-        h_codes = [[keep.tile([P, PAIR], U32, name="h_codes%d_%d" % (o, g), align_bytes=64) for g in range(2)] for o in range(PASSES)]
-        h_plane = [[keep.tile([P, PAIR], U8, name="h_plane%d_%d" % (o, g), align_bytes=64) for g in range(2)] for o in range(PASSES)]
-        copied = {(m, c.start): keep.tile([P, HALF], F32, name="copied%d_%d" % (m, c.start), tag="copied%d_%d" % (m, c.start), align_bytes=64) for m, c in aside}
+        h_bf16 = [[keep.tile([P, PAIR * PACK], BF16, name="h_bf16_%d_%d" % (o, g), align_bytes=64) for g in range(PAIRS)] for o in range(PASSES)]
+        h_codes = [[keep.tile([P, PAIR], U32, name="h_codes%d_%d" % (o, g), align_bytes=64) for g in range(PAIRS)] for o in range(PASSES)]
+        h_plane = [[keep.tile([P, PAIR], U8, name="h_plane%d_%d" % (o, g), align_bytes=64) for g in range(PAIRS)] for o in range(PASSES)]
+        copied = {(m, c.start): keep.tile([P, c.stop - c.start], F32, name="copied%d_%d" % (m, c.start), align_bytes=64) for m, c in aside}
         gap = [keep.tile([P, S], F32, name="gap%d" % m, tag="gap%d" % m, align_bytes=64) for m in range(TILES)]
-        neg = gap[:2] + [keep.tile([P, S], F32, name="neg%d" % m, tag="gap%d" % (m % 2), align_bytes=64) for m in range(2, TILES)]
-        e = [keep.tile([P, S], F32, name="e%d" % m) for m in range(TILES)]
+        gap4 = gap[:2] + [keep.tile([P, S], F32, name="gap4_%d" % m, tag="gap%d" % (m - 2), align_bytes=64) for m in (2, 3)]
+        expo = [keep.tile([P, S], F32, name="expo%d" % m) for m in range(TILES)]
         prob = [keep.tile([P, S], F32, name="prob%d" % m) for m in range(TILES)]
         low = [keep.tile([P, 1], F32, name="low%d" % m) for m in range(TILES)]
         total = [keep.tile([P, 1], F32, name="total%d" % m) for m in range(TILES)]
@@ -92,15 +94,15 @@ def tile_picked_zams_soft_p_kernel(tc, x_words, x_scales, hT, label, offs, out):
 
         def interleave(o, g):
             raw = h_raw[o][:, :, g * PAIR : (g + 1) * PAIR]
-            dst = stage[o][g][:].rearrange("p (c i j) -> p c j i", i=PACK, j=PACK)
-            src = raw.rearrange("p j (c i) -> p c j i", i=PACK)
+            dst = h_bf16[o][g][:].rearrange("p (c i r) -> p c r i", i=PACK, r=PACK)
+            src = raw.rearrange("p r (c i) -> p c r i", i=PACK)
             if g == 0:
                 nc.vector.tensor_scalar(dst, src, SCALE, None, ALU.mult)
             else:
-                nc.scalar.activation(dst, src, ACT.Copy, scale=SCALE)
+                nc.scalar.activation(dst, src, ACT.Copy)
 
         def quantize(o, g):
-            nc.vector.quantize_mx(out=h_codes[o][g][:].bitcast(FP8X4), scales=h_plane[o][g][:], in_=stage[o][g][:])
+            nc.vector.quantize_mx(out=h_codes[o][g][:].bitcast(FP8X4), scales=h_plane[o][g][:], in_=h_bf16[o][g][:])
 
         def multiply(m, c, o):
             faces = slice((m % 2) * P, (m % 2 + 1) * P)
@@ -117,82 +119,70 @@ def tile_picked_zams_soft_p_kernel(tc, x_words, x_scales, hT, label, offs, out):
         def score(m, c):
             return scores[m, 0][:, c] if m == TILES - 1 else scores[m, c.start][:]
 
-        def subtract(m, c):
-            if m < 2:
-                nc.vector.scalar_tensor_tensor(gap[m][:, c], margin[m][:, c], SCALE, score(m, c), ALU.mult, ALU.subtract)
-            else:
-                nc.vector.scalar_tensor_tensor(gap[m][:, c], score(m, c), -1.0 / SCALE, margin[m][:, c], ALU.mult, ALU.add)
-
-        def subtract_aside(m, c):
-            nc.scalar.activation(copied[m, c.start][:], score(m, c), ACT.Copy, scale=1.0 / SCALE)
-            nc.gpsimd.tensor_tensor(gap[m][:, c], margin[m][:, c], copied[m, c.start][:], ALU.subtract)
-
-        def lowest(m):
-            if m < 2:
-                nc.vector.tensor_reduce(low[m][:], gap[m][:], mybir.AxisListType.X, ALU.min)
-            else:
-                nc.vector.tensor_scalar(neg[m][:], gap[m][:], SCALE, None, ALU.mult, ALU.min, accum_out=low[m][:])
-
         def exponent(m):
-            nc.scalar.activation(e[m][:], neg[m][:], ACT.Exp, bias=low[m][:], scale=-1.0, accum_out=total[m][:])
+            nc.scalar.activation(expo[m][:], gap4[m][:], ACT.Exp, bias=low[m][:], scale=-1.0, accum_out=total[m][:])
+
+        def scaled_minimum(m):
+            nc.vector.tensor_scalar(gap4[m][:], gap[m][:], SCALE, None, ALU.mult, ALU.min, accum_out=low[m][:])
 
         def invert(m):
             nc.vector.reciprocal(inv[m][:], total[m][:])
 
         def normalise(m, c):
-            nc.vector.tensor_scalar(prob[m][:, c], e[m][:, c], inv[m][:], None, ALU.mult)
+            nc.vector.tensor_scalar(prob[m][:, c], expo[m][:, c], inv[m][:], None, ALU.mult)
 
-        def normalise_aside(m, c):
-            nc.gpsimd.tensor_scalar(prob[m][:, c], e[m][:, c], inv[m][:], 0.0, ALU.mult, ALU.add)
+        def normalise_on_gpsimd(m, c):
+            nc.gpsimd.tensor_scalar(prob[m][:, c], expo[m][:, c], inv[m][:], 0.0, ALU.mult, ALU.add)
 
         def store(m, c):
             nc.sync.dma_start(out=out[m * P : (m + 1) * P, c], in_=prob[m][:, c])
 
         gather_words(0, WHOLE)
-        for g in range(2):
+        for g in range(PAIRS):
             interleave(0, g)
-        margins = keep.tile([P, TILES, S], F32, name="margins", tag="raw0", align_bytes=64)
-        margin = [margins[:, m, :] for m in range(TILES)]
+        margin = keep.tile([P, TILES, S], F32, name="margin", tag="raw0", align_bytes=64)
         for m in range(TILES):
-            nc.sync.dma_start(out=margin[m], in_=label[m * P : (m + 1) * P, :])
-        for g in range(2):
+            nc.sync.dma_start(out=margin[:, m, :], in_=label[m * P : (m + 1) * P, :])
+        for g in range(PAIRS):
             quantize(0, g)
-        for g in range(2):
+        for g in range(PAIRS):
             interleave(1, g)
-        for g in range(2):
+        for g in range(PAIRS):
             quantize(1, g)
         for m, c in pieces:
             multiply(m, c, 0)
-        for c in HALVES:
+        for c in (FRONT, BACK):
             gather_words(1, c)
         for m, c in pieces:
             multiply(m, c, 1)
 
-        for c in HALVES:
-            for m in range(2):
-                subtract(m, c)
+        for c in (FRONT, BACK):
+            for m in (0, 1):
+                nc.vector.scalar_tensor_tensor(gap4[m][:, c], margin[:, m, c], SCALE, score(m, c), ALU.mult, ALU.subtract)
         for m, c in aside:
-            subtract_aside(m, c)
-        for m in range(2):
-            lowest(m)
+            nc.scalar.activation(copied[m, c.start][:], score(m, c), ACT.Copy)
+            nc.gpsimd.tensor_tensor(gap[m][:, c], margin[:, m, c], copied[m, c.start][:], ALU.subtract)
+        for m in (0, 1):
+            nc.vector.tensor_reduce(low[m][:], gap4[m][:], mybir.AxisListType.X, ALU.min)
             exponent(m)
-        subtract(3, HALVES[1])
+        nc.vector.tensor_tensor(gap[3][:, BACK], margin[:, 3, BACK], score(3, BACK), ALU.subtract)
+
         invert(0)
-        normalise_aside(0, HALVES[0])
-        nc.scalar.activation(prob[0][:, HALVES[1]], e[0][:, HALVES[1]], ACT.Copy, scale=inv[0][:])
+        normalise_on_gpsimd(0, FRONT)
+        nc.scalar.activation(prob[0][:, BACK], expo[0][:, BACK], ACT.Copy, scale=inv[0][:])
         store(0, WHOLE)
-        lowest(2)
+        scaled_minimum(2)
         exponent(2)
         invert(1)
-        normalise_aside(1, HALVES[0])
-        lowest(3)
+        normalise_on_gpsimd(1, FRONT)
+        scaled_minimum(3)
         exponent(3)
         invert(2)
-        normalise(1, HALVES[1])
+        normalise(1, BACK)
         store(1, WHOLE)
         normalise(2, WHOLE)
         store(2, WHOLE)
         invert(3)
-        for c in HALVES:
+        for c in (FRONT, BACK):
             normalise(3, c)
             store(3, c)

@@ -36,12 +36,14 @@ def tile_picked_zams_soft_p_kernel(tc, x_words, x_scales, hT, label, offs, out):
     nc = tc.nc
     with ExitStack() as ctx:
         keep = ctx.enter_context(tc.tile_pool(name="keep", bufs=1))
+        shared = ctx.enter_context(tc.tile_pool(name="shared", bufs=1))
         psum = ctx.enter_context(tc.psum_pool(name="psum", bufs=1))
 
         offsets = keep.tile([P, S // LIST_ROWS], U16, name="offsets")
-        scale_table = keep.tile([P, T], U8, name="scale_table", tag="words1", align_bytes=64)
-        word_table = [keep.tile([P, T], I32, name="word_table%d" % o, tag="words%d" % o, align_bytes=64) for o in range(PASSES)]
-        h_raw = [keep.tile([P, PACK, J], F32, name="h_raw%d" % o, tag="raw%d" % o, align_bytes=64) for o in range(PASSES)]
+        scale_table = shared.tile([P, T], U8, name="scale_table", offset=4 * T - T // 2)
+        word_table = [keep.tile([P, T], I32, name="word_table0", align_bytes=64), shared.tile([P, T], I32, name="word_table1", offset=0)]
+        h_second = [keep.tile([P, PACK, PAIR], F32, name="h_second0", align_bytes=64), shared.tile([P, PACK, PAIR], F32, name="h_second1", offset=4 * T)]
+        h_first = keep.tile([P, PACK, J], F32, name="h_first", tag="first", align_bytes=64)
         x_scales_picked = keep.tile([P, S], U8, name="x_scales_picked", align_bytes=64)
         x_planes = keep.tile([P, PASSES * S], U8, name="x_planes", align_bytes=64)
 
@@ -52,17 +54,15 @@ def tile_picked_zams_soft_p_kernel(tc, x_words, x_scales, hT, label, offs, out):
             words = x_words[o].rearrange("p n t -> p (n t)").bitcast(I32)
             nc.sync.dma_start(out=word_table[o][:, columns], in_=words[:, columns])
 
-        def load_h(o):
-            rows = hT[o * K_PASS : (o + 1) * K_PASS, :]
-            nc.sync.dma_start(out=h_raw[o][:], in_=rows.rearrange("(p r) c -> p r c", r=PACK))
+        def h_rows(o):
+            return hT[o * K_PASS : (o + 1) * K_PASS, :].rearrange("(p r) c -> p r c", r=PACK)
 
         load_words(0, slice(0, T // 2))
         nc.sync.dma_start(offsets[:], offs)
-        for o in range(PASSES):
-            nc.sync.dma_start(out=scale_table[SPREAD * o :: SPREAD * PASSES, :].bitcast(I32), in_=x_scales[o].bitcast(I32))
+        nc.sync.dma_start(out=scale_table[::SPREAD, :].bitcast(I32), in_=x_scales.bitcast(I32).rearrange("o i c -> i o c"))
         load_words(0, slice(T // 2, T))
-        for o in range(PASSES):
-            load_h(o)
+        nc.sync.dma_start(out=h_first[:], in_=h_rows(0))
+        nc.sync.dma_start(out=h_second[0][:], in_=h_rows(1)[:, :, :PAIR])
         nc.vector.tensor_copy(x_scales_picked[:], scale_table[:].indirect(offsets[:]))
         for q in range(QUADRANTS):
             first = QUADRANT * q
@@ -71,53 +71,62 @@ def tile_picked_zams_soft_p_kernel(tc, x_words, x_scales, hT, label, offs, out):
                 in_=x_scales_picked[first : first + QUADRANT : SPREAD, :].bitcast(I32),
             )
         load_words(1, slice(0, T))
+        nc.sync.dma_start(out=h_second[1][:], in_=h_rows(1)[:, :, PAIR:])
 
-        pieces = [(m, c) for c in (FRONT, BACK) for m in (0, 2, 1)] + [(3, WHOLE)]
-        aside = [(2, FRONT), (2, BACK), (3, FRONT)]
         x_codes = [keep.tile([P, S], U32, name="x_codes%d" % o, align_bytes=64) for o in range(PASSES)]
-        scores = {(m, c.start): psum.tile([P, c.stop - c.start], F32, name="scores%d_%d" % (m, c.start)) for m, c in pieces}
-        h_bf16 = [[keep.tile([P, PAIR * PACK], BF16, name="h_bf16_%d_%d" % (o, g), align_bytes=64) for g in range(PAIRS)] for o in range(PASSES)]
-        h_codes = [[keep.tile([P, PAIR], U32, name="h_codes%d_%d" % (o, g), align_bytes=64) for g in range(PAIRS)] for o in range(PASSES)]
-        h_plane = [[keep.tile([P, PAIR], U8, name="h_plane%d_%d" % (o, g), align_bytes=64) for g in range(PAIRS)] for o in range(PASSES)]
-        copied = {(m, c.start): keep.tile([P, c.stop - c.start], F32, name="copied%d_%d" % (m, c.start), align_bytes=64) for m, c in aside}
-        gap = [keep.tile([P, S], F32, name="gap%d" % m, tag="gap%d" % m, align_bytes=64) for m in range(TILES)]
-        gap4 = gap[:2] + [keep.tile([P, S], F32, name="gap4_%d" % m, tag="gap%d" % (m - 2), align_bytes=64) for m in (2, 3)]
+        scores = [psum.tile([P, S], F32, name="scores%d" % m) for m in range(TILES)]
+        h_bf16 = [[keep.tile([P, P * PACK], BF16, name="h_bf16_%d_%d" % (o, m), align_bytes=64) for m in range(TILES)] for o in range(PASSES)]
+        h_codes = [[keep.tile([P, P], U32, name="h_codes%d_%d" % (o, m), align_bytes=64) for m in range(TILES)] for o in range(PASSES)]
+        h_plane = [[keep.tile([P, P], U8, name="h_plane%d_%d" % (o, m), align_bytes=64) for m in range(TILES)] for o in range(PASSES)]
+        aside = [(1, FRONT), (3, WHOLE)]
+        copied = {m: keep.tile([P, c.stop - c.start], F32, name="copied%d" % m, align_bytes=64) for m, c in aside[1:]}
+        copied[1] = shared.tile([P, S // 2], F32, name="copied1_shared", offset=4 * T)
+        gap = [keep.tile([P, S], F32, name="gap%d" % m, tag="gap%d" % m, align_bytes=64) if m else None for m in range(TILES)]
+        gap[0] = shared.tile([P, S], F32, name="gap0_shared", offset=4 * T + T)
+        gap4 = {0: gap[0], 2: gap[2]}
+        for m in (1, 3):
+            gap4[m] = keep.tile([P, S], F32, name="gap4_%d" % m, tag="gap4", align_bytes=64)
         expo = [keep.tile([P, S], F32, name="expo%d" % m) for m in range(TILES)]
         prob = [keep.tile([P, S], F32, name="prob%d" % m) for m in range(TILES)]
-        low = [keep.tile([P, 1], F32, name="low%d" % m) for m in range(TILES)]
+        low = [keep.tile([P, 1], F32, name="low%d" % m) if m != 2 else None for m in range(TILES)]
+        low[2] = shared.tile([P, 1], F32, name="low2_shared", offset=4 * T + T)
         total = [keep.tile([P, 1], F32, name="total%d" % m) for m in range(TILES)]
         inv = [keep.tile([P, 1], F32, name="inv%d" % m) for m in range(TILES)]
 
-        def gather_words(o, c):
-            part = offsets[:, c.start // LIST_ROWS : c.stop // LIST_ROWS]
-            nc.vector.tensor_copy(x_codes[o][:, c], word_table[o][:].bitcast(U32).indirect(part))
+        def gather_words(o):
+            nc.vector.tensor_copy(x_codes[o][:], word_table[o][:].bitcast(U32).indirect(offsets[:]))
 
-        def interleave(o, g):
-            raw = h_raw[o][:, :, g * PAIR : (g + 1) * PAIR]
-            dst = h_bf16[o][g][:].rearrange("p (c i r) -> p c r i", i=PACK, r=PACK)
+        def interleave(o, m):
+            if o == 0:
+                raw = h_first[:, :, m * P : (m + 1) * P]
+            else:
+                raw = h_second[m // 2][:, :, (m % 2) * P : (m % 2 + 1) * P]
+            dst = h_bf16[o][m][:].rearrange("p (c i r) -> p c r i", i=PACK, r=PACK)
             src = raw.rearrange("p r (c i) -> p c r i", i=PACK)
-            if g == 0:
+            if m % 2 == 0:
                 nc.vector.tensor_scalar(dst, src, SCALE, None, ALU.mult)
             else:
                 nc.scalar.activation(dst, src, ACT.Copy)
 
-        def quantize(o, g):
-            nc.vector.quantize_mx(out=h_codes[o][g][:].bitcast(FP8X4), scales=h_plane[o][g][:], in_=h_bf16[o][g][:])
+        def quantize(o, m):
+            nc.vector.quantize_mx(out=h_codes[o][m][:].bitcast(FP8X4), scales=h_plane[o][m][:], in_=h_bf16[o][m][:])
 
-        def multiply(m, c, o):
-            faces = slice((m % 2) * P, (m % 2 + 1) * P)
+        def multiply(m, o):
             nc.tensor.matmul_mx(
-                out=scores[m, c.start][:],
-                lhsT=h_codes[o][m // 2][:, faces].bitcast(FP8X4),
-                lhsT_scale=h_plane[o][m // 2][:, faces],
-                rhs=x_codes[o][:, c].bitcast(FP8X4),
-                rhs_scale=x_planes[:, o * S + c.start : o * S + c.stop],
+                out=scores[m][:],
+                lhsT=h_codes[o][m][:].bitcast(FP8X4),
+                lhsT_scale=h_plane[o][m][:],
+                rhs=x_codes[o][:].bitcast(FP8X4),
+                rhs_scale=x_planes[:, o * S : (o + 1) * S],
                 start=(o == 0),
                 stop=(o == PASSES - 1),
             )
 
-        def score(m, c):
-            return scores[m, 0][:, c] if m == TILES - 1 else scores[m, c.start][:]
+        def subtract(m):
+            nc.vector.scalar_tensor_tensor(gap4[m][:], margin[:, m, :], SCALE, scores[m][:], ALU.mult, ALU.subtract)
+
+        def minimum(m):
+            nc.vector.tensor_reduce(low[m][:], gap4[m][:], mybir.AxisListType.X, ALU.min)
 
         def exponent(m):
             nc.scalar.activation(expo[m][:], gap4[m][:], ACT.Exp, bias=low[m][:], scale=-1.0, accum_out=total[m][:])
@@ -137,49 +146,48 @@ def tile_picked_zams_soft_p_kernel(tc, x_words, x_scales, hT, label, offs, out):
         def store(m, c):
             nc.sync.dma_start(out=out[m * P : (m + 1) * P, c], in_=prob[m][:, c])
 
-        gather_words(0, WHOLE)
-        for g in range(PAIRS):
-            interleave(0, g)
-        margin = keep.tile([P, TILES, S], F32, name="margin", tag="raw0", align_bytes=64)
+        gather_words(0)
+        for m in range(TILES):
+            interleave(0, m)
+        margin = keep.tile([P, TILES, S], F32, name="margin", tag="first", align_bytes=64)
         for m in range(TILES):
             nc.sync.dma_start(out=margin[:, m, :], in_=label[m * P : (m + 1) * P, :])
+        for m in range(TILES):
+            quantize(0, m)
+        for m in range(TILES):
+            multiply(m, 0)
         for g in range(PAIRS):
-            quantize(0, g)
-        for g in range(PAIRS):
-            interleave(1, g)
-        for g in range(PAIRS):
-            quantize(1, g)
-        for m, c in pieces:
-            multiply(m, c, 0)
-        for c in (FRONT, BACK):
-            gather_words(1, c)
-        for m, c in pieces:
-            multiply(m, c, 1)
+            for m in (2 * g, 2 * g + 1):
+                interleave(1, m)
+            for m in (2 * g, 2 * g + 1):
+                quantize(1, m)
+            if g == 0:
+                gather_words(1)
+            for m in (2 * g, 2 * g + 1):
+                multiply(m, 1)
 
-        for c in (FRONT, BACK):
-            for m in (0, 1):
-                nc.vector.scalar_tensor_tensor(gap4[m][:, c], margin[:, m, c], SCALE, score(m, c), ALU.mult, ALU.subtract)
+        subtract(0)
         for m, c in aside:
-            nc.scalar.activation(copied[m, c.start][:], score(m, c), ACT.Copy)
-            nc.gpsimd.tensor_tensor(gap[m][:, c], margin[:, m, c], copied[m, c.start][:], ALU.subtract)
-        for m in (0, 1):
-            nc.vector.tensor_reduce(low[m][:], gap4[m][:], mybir.AxisListType.X, ALU.min)
-            exponent(m)
-        nc.vector.tensor_tensor(gap[3][:, BACK], margin[:, 3, BACK], score(3, BACK), ALU.subtract)
-
+            nc.scalar.activation(copied[m][:], scores[m][:, c], ACT.Copy)
+            nc.gpsimd.tensor_tensor(gap[m][:, c], margin[:, m, c], copied[m][:], ALU.subtract)
+        nc.vector.tensor_tensor(gap[1][:, BACK], margin[:, 1, BACK], scores[1][:, BACK], ALU.subtract)
+        minimum(0)
+        exponent(0)
+        scaled_minimum(1)
+        exponent(1)
+        subtract(2)
         invert(0)
         normalise_on_gpsimd(0, FRONT)
         nc.scalar.activation(prob[0][:, BACK], expo[0][:, BACK], ACT.Copy, scale=inv[0][:])
         store(0, WHOLE)
-        scaled_minimum(2)
+        minimum(2)
         exponent(2)
         invert(1)
-        normalise_on_gpsimd(1, FRONT)
+        normalise_on_gpsimd(1, WHOLE)
+        store(1, WHOLE)
         scaled_minimum(3)
         exponent(3)
         invert(2)
-        normalise(1, BACK)
-        store(1, WHOLE)
         normalise(2, WHOLE)
         store(2, WHOLE)
         invert(3)

@@ -42,7 +42,8 @@ def tile_picked_zams_soft_p_kernel(tc, x_words, x_scales, hT, label, offs, out):
         offsets = keep.tile([P, S // LIST_ROWS], U16, name="offsets")
         scale_table = shared.tile([P, T], U8, name="scale_table", offset=4 * T - T // 2)
         word_table = [keep.tile([P, T], I32, name="word_table0", align_bytes=64), shared.tile([P, T], I32, name="word_table1", offset=0)]
-        h_second = [keep.tile([P, PACK, PAIR], F32, name="h_second0", align_bytes=64), shared.tile([P, PACK, PAIR], F32, name="h_second1", offset=4 * T)]
+        h_halves = shared.tile([P, PAIRS, PACK, PAIR], F32, name="h_halves", offset=4 * T)
+        h_second = [h_halves[:, g] for g in range(PAIRS)]
         h_first = keep.tile([P, PACK, J], F32, name="h_first", tag="first", align_bytes=64)
         x_scales_picked = keep.tile([P, S], U8, name="x_scales_picked", align_bytes=64)
         x_planes = keep.tile([P, PASSES * S], U8, name="x_planes", align_bytes=64)
@@ -57,12 +58,11 @@ def tile_picked_zams_soft_p_kernel(tc, x_words, x_scales, hT, label, offs, out):
         def h_rows(o):
             return hT[o * K_PASS : (o + 1) * K_PASS, :].rearrange("(p r) c -> p r c", r=PACK)
 
-        load_words(0, slice(0, T // 2))
+        load_words(0, slice(0, T // 4))
         nc.sync.dma_start(offsets[:], offs)
         nc.sync.dma_start(out=scale_table[::SPREAD, :].bitcast(I32), in_=x_scales.bitcast(I32).rearrange("o i c -> i o c"))
-        load_words(0, slice(T // 2, T))
+        load_words(0, slice(T // 4, T))
         nc.sync.dma_start(out=h_first[:], in_=h_rows(0))
-        nc.sync.dma_start(out=h_second[0][:], in_=h_rows(1)[:, :, :PAIR])
         nc.vector.tensor_copy(x_scales_picked[:], scale_table[:].indirect(offsets[:]))
         for q in range(QUADRANTS):
             first = QUADRANT * q
@@ -71,7 +71,8 @@ def tile_picked_zams_soft_p_kernel(tc, x_words, x_scales, hT, label, offs, out):
                 in_=x_scales_picked[first : first + QUADRANT : SPREAD, :].bitcast(I32),
             )
         load_words(1, slice(0, T))
-        nc.sync.dma_start(out=h_second[1][:], in_=h_rows(1)[:, :, PAIR:])
+        for g in range(PAIRS):
+            nc.sync.dma_start(out=h_second[g], in_=h_rows(1)[:, :, g * PAIR : (g + 1) * PAIR])
 
         x_codes = [keep.tile([P, S], U32, name="x_codes%d" % o, align_bytes=64) for o in range(PASSES)]
         scores = [psum.tile([P, S], F32, name="scores%d" % m) for m in range(TILES)]
@@ -156,13 +157,12 @@ def tile_picked_zams_soft_p_kernel(tc, x_words, x_scales, hT, label, offs, out):
             quantize(0, m)
         for m in range(TILES):
             multiply(m, 0)
+        gather_words(1)
         for g in range(PAIRS):
             for m in (2 * g, 2 * g + 1):
                 interleave(1, m)
             for m in (2 * g, 2 * g + 1):
                 quantize(1, m)
-            if g == 0:
-                gather_words(1)
             for m in (2 * g, 2 * g + 1):
                 multiply(m, 1)
 

@@ -18,6 +18,10 @@ LIST_ROWS = 16
 SCALE = 4.0
 FLOPS = 2 * K * J * S
 
+HEAD = T // 4
+TABLE_BYTES = 4 * T
+ROW_BYTES = 4 * S
+
 WHOLE = slice(0, S)
 FRONT, BACK = slice(0, S // 2), slice(S // 2, S)
 
@@ -40,10 +44,9 @@ def tile_picked_zams_soft_p_kernel(tc, x_words, x_scales, hT, label, offs, out):
         psum = ctx.enter_context(tc.psum_pool(name="psum", bufs=1))
 
         offsets = keep.tile([P, S // LIST_ROWS], U16, name="offsets")
-        scale_table = shared.tile([P, T], U8, name="scale_table", offset=4 * T - T // 2)
+        scale_table = shared.tile([P, T], U8, name="scale_table", offset=TABLE_BYTES - T // 2)
         word_table = [keep.tile([P, T], I32, name="word_table0", align_bytes=64), shared.tile([P, T], I32, name="word_table1", offset=0)]
-        h_halves = shared.tile([P, PAIRS, PACK, PAIR], F32, name="h_halves", offset=4 * T)
-        h_second = [h_halves[:, g] for g in range(PAIRS)]
+        h_second = shared.tile([P, PAIRS, PACK, PAIR], F32, name="h_second", offset=TABLE_BYTES)
         h_first = keep.tile([P, PACK, J], F32, name="h_first", tag="first", align_bytes=64)
         x_scales_picked = keep.tile([P, S], U8, name="x_scales_picked", align_bytes=64)
         x_planes = keep.tile([P, PASSES * S], U8, name="x_planes", align_bytes=64)
@@ -58,21 +61,21 @@ def tile_picked_zams_soft_p_kernel(tc, x_words, x_scales, hT, label, offs, out):
         def h_rows(o):
             return hT[o * K_PASS : (o + 1) * K_PASS, :].rearrange("(p r) c -> p r c", r=PACK)
 
-        load_words(0, slice(0, T // 4))
+        load_words(0, slice(0, HEAD))
         nc.sync.dma_start(offsets[:], offs)
         nc.sync.dma_start(out=scale_table[::SPREAD, :].bitcast(I32), in_=x_scales.bitcast(I32).rearrange("o i c -> i o c"))
-        load_words(0, slice(T // 4, T))
+        load_words(0, slice(HEAD, T))
         nc.sync.dma_start(out=h_first[:], in_=h_rows(0))
         nc.vector.tensor_copy(x_scales_picked[:], scale_table[:].indirect(offsets[:]))
         for q in range(QUADRANTS):
             first = QUADRANT * q
-            nc.sync.dma_start(
+            (nc.sync, nc.scalar)[q % 2].dma_start(
                 out=x_planes[first : first + PLANE_ROWS, :].bitcast(I32),
                 in_=x_scales_picked[first : first + QUADRANT : SPREAD, :].bitcast(I32),
             )
         load_words(1, slice(0, T))
         for g in range(PAIRS):
-            nc.sync.dma_start(out=h_second[g], in_=h_rows(1)[:, :, g * PAIR : (g + 1) * PAIR])
+            nc.sync.dma_start(out=h_second[:, g], in_=h_rows(1)[:, :, g * PAIR : (g + 1) * PAIR])
 
         x_codes = [keep.tile([P, S], U32, name="x_codes%d" % o, align_bytes=64) for o in range(PASSES)]
         scores = [psum.tile([P, S], F32, name="scores%d" % m) for m in range(TILES)]
@@ -80,17 +83,20 @@ def tile_picked_zams_soft_p_kernel(tc, x_words, x_scales, hT, label, offs, out):
         h_codes = [[keep.tile([P, P], U32, name="h_codes%d_%d" % (o, m), align_bytes=64) for m in range(TILES)] for o in range(PASSES)]
         h_plane = [[keep.tile([P, P], U8, name="h_plane%d_%d" % (o, m), align_bytes=64) for m in range(TILES)] for o in range(PASSES)]
         aside = [(1, FRONT), (3, WHOLE)]
-        copied = {m: keep.tile([P, c.stop - c.start], F32, name="copied%d" % m, align_bytes=64) for m, c in aside[1:]}
-        copied[1] = shared.tile([P, S // 2], F32, name="copied1_shared", offset=4 * T)
-        gap = [keep.tile([P, S], F32, name="gap%d" % m, tag="gap%d" % m, align_bytes=64) if m else None for m in range(TILES)]
-        gap[0] = shared.tile([P, S], F32, name="gap0_shared", offset=4 * T + T)
-        gap4 = {0: gap[0], 2: gap[2]}
+        copied = {
+            3: keep.tile([P, S], F32, name="copied3", align_bytes=64),
+            1: shared.tile([P, S // 2], F32, name="copied1", offset=TABLE_BYTES),
+        }
+        differences = {m: keep.tile([P, S], F32, name="difference%d" % m, align_bytes=64) for m in (1, 2, 3)}
+        differences[0] = shared.tile([P, S], F32, name="difference0", offset=TABLE_BYTES + ROW_BYTES)
+        gap = {m: differences[m] for m in (1, 3)}
+        gap4 = {m: differences[m] for m in (0, 2)}
         for m in (1, 3):
-            gap4[m] = keep.tile([P, S], F32, name="gap4_%d" % m, tag="gap4", align_bytes=64)
+            gap4[m] = keep.tile([P, S], F32, name="gap4_%d" % m, tag="gap4_odd", align_bytes=64)
         expo = [keep.tile([P, S], F32, name="expo%d" % m) for m in range(TILES)]
         prob = [keep.tile([P, S], F32, name="prob%d" % m) for m in range(TILES)]
-        low = [keep.tile([P, 1], F32, name="low%d" % m) if m != 2 else None for m in range(TILES)]
-        low[2] = shared.tile([P, 1], F32, name="low2_shared", offset=4 * T + T)
+        low = {m: keep.tile([P, 1], F32, name="low%d" % m) for m in (0, 1, 3)}
+        low[2] = shared.tile([P, 1], F32, name="low2", offset=TABLE_BYTES + ROW_BYTES)
         total = [keep.tile([P, 1], F32, name="total%d" % m) for m in range(TILES)]
         inv = [keep.tile([P, 1], F32, name="inv%d" % m) for m in range(TILES)]
 
@@ -101,10 +107,14 @@ def tile_picked_zams_soft_p_kernel(tc, x_words, x_scales, hT, label, offs, out):
             if o == 0:
                 raw = h_first[:, :, m * P : (m + 1) * P]
             else:
-                raw = h_second[m // 2][:, :, (m % 2) * P : (m % 2 + 1) * P]
+                raw = h_second[:, m // 2, :, (m % 2) * P : (m % 2 + 1) * P]
             dst = h_bf16[o][m][:].rearrange("p (c i r) -> p c r i", i=PACK, r=PACK)
             src = raw.rearrange("p r (c i) -> p c r i", i=PACK)
-            if m % 2 == 0:
+            if (o, m) == (1, 3):
+                nc.vector.tensor_copy(dst, src)
+            elif (o, m) == (1, 2):
+                nc.scalar.activation(dst, src, ACT.Copy, scale=SCALE)
+            elif m % 2 == 0:
                 nc.vector.tensor_scalar(dst, src, SCALE, None, ALU.mult)
             else:
                 nc.scalar.activation(dst, src, ACT.Copy)
@@ -129,11 +139,11 @@ def tile_picked_zams_soft_p_kernel(tc, x_words, x_scales, hT, label, offs, out):
         def minimum(m):
             nc.vector.tensor_reduce(low[m][:], gap4[m][:], mybir.AxisListType.X, ALU.min)
 
-        def exponent(m):
-            nc.scalar.activation(expo[m][:], gap4[m][:], ACT.Exp, bias=low[m][:], scale=-1.0, accum_out=total[m][:])
-
         def scaled_minimum(m):
             nc.vector.tensor_scalar(gap4[m][:], gap[m][:], SCALE, None, ALU.mult, ALU.min, accum_out=low[m][:])
+
+        def exponent(m):
+            nc.scalar.activation(expo[m][:], gap4[m][:], ACT.Exp, bias=low[m][:], scale=-1.0, accum_out=total[m][:])
 
         def invert(m):
             nc.vector.reciprocal(inv[m][:], total[m][:])
@@ -151,19 +161,19 @@ def tile_picked_zams_soft_p_kernel(tc, x_words, x_scales, hT, label, offs, out):
         for m in range(TILES):
             interleave(0, m)
         margin = keep.tile([P, TILES, S], F32, name="margin", tag="first", align_bytes=64)
-        for m in range(TILES):
+        for m in (0, 1, 3, 2):
             nc.sync.dma_start(out=margin[:, m, :], in_=label[m * P : (m + 1) * P, :])
         for m in range(TILES):
             quantize(0, m)
         for m in range(TILES):
             multiply(m, 0)
         gather_words(1)
-        for g in range(PAIRS):
-            for m in (2 * g, 2 * g + 1):
+        for pair in ((0, 1), (3, 2)):
+            for m in pair:
                 interleave(1, m)
-            for m in (2 * g, 2 * g + 1):
+            for m in pair:
                 quantize(1, m)
-            for m in (2 * g, 2 * g + 1):
+            for m in pair:
                 multiply(m, 1)
 
         subtract(0)
@@ -176,6 +186,7 @@ def tile_picked_zams_soft_p_kernel(tc, x_words, x_scales, hT, label, offs, out):
         scaled_minimum(1)
         exponent(1)
         subtract(2)
+
         invert(0)
         normalise_on_gpsimd(0, FRONT)
         nc.scalar.activation(prob[0][:, BACK], expo[0][:, BACK], ACT.Copy, scale=inv[0][:])

@@ -194,11 +194,13 @@ def tile_picked_zams_soft_p_kernel(tc, x_words, x_scales, hT, label, offs, out):
         minimum(2)
         exponent(2)
         invert(1)
-        normalise_on_gpsimd(1, WHOLE)
-        store(1, WHOLE)
+        normalise_on_gpsimd(1, FRONT)
+        store(1, FRONT)
         scaled_minimum(3)
         exponent(3)
         invert(2)
+        normalise(1, BACK)
+        store(1, BACK)
         normalise(2, WHOLE)
         store(2, WHOLE)
         invert(3)

@@ -87,16 +87,16 @@ def tile_picked_zams_soft_p_kernel(tc, x_words, x_scales, hT, label, offs, out):
             3: keep.tile([P, S], F32, name="copied3", align_bytes=64),
             1: shared.tile([P, S // 2], F32, name="copied1", offset=TABLE_BYTES),
         }
-        differences = {m: keep.tile([P, S], F32, name="difference%d" % m, align_bytes=64) for m in (1, 2, 3)}
+        differences = {m: keep.tile([P, S], F32, name="difference%d" % m, tag="difference%d" % m, align_bytes=64) for m in (1, 2, 3)}
         differences[0] = shared.tile([P, S], F32, name="difference0", offset=TABLE_BYTES + ROW_BYTES)
         gap = {m: differences[m] for m in (1, 3)}
         gap4 = {m: differences[m] for m in (0, 2)}
-        for m in (1, 3):
-            gap4[m] = keep.tile([P, S], F32, name="gap4_%d" % m, tag="gap4_odd", align_bytes=64)
+        gap4[3] = keep.tile([P, S], F32, name="gap4_3", tag="difference1", align_bytes=64)
         expo = [keep.tile([P, S], F32, name="expo%d" % m) for m in range(TILES)]
         prob = [keep.tile([P, S], F32, name="prob%d" % m) for m in range(TILES)]
         low = {m: keep.tile([P, 1], F32, name="low%d" % m) for m in (0, 1, 3)}
         low[2] = shared.tile([P, 1], F32, name="low2", offset=TABLE_BYTES + ROW_BYTES)
+        low_gap = keep.tile([P, 1], F32, name="low_gap")
         total = [keep.tile([P, 1], F32, name="total%d" % m) for m in range(TILES)]
         inv = [keep.tile([P, 1], F32, name="inv%d" % m) for m in range(TILES)]
 
@@ -183,8 +183,9 @@ def tile_picked_zams_soft_p_kernel(tc, x_words, x_scales, hT, label, offs, out):
         nc.vector.tensor_tensor(gap[1][:, BACK], margin[:, 1, BACK], scores[1][:, BACK], ALU.subtract)
         minimum(0)
         exponent(0)
-        scaled_minimum(1)
-        exponent(1)
+        nc.vector.tensor_reduce(low_gap[:], gap[1][:], mybir.AxisListType.X, ALU.min)
+        nc.scalar.activation(low[1][:], low_gap[:], ACT.Copy, scale=SCALE)
+        nc.scalar.activation(expo[1][:], gap[1][:], ACT.Exp, bias=low[1][:], scale=-SCALE, accum_out=total[1][:])
         subtract(2)
 
         invert(0)

from contextlib import ExitStack

import concourse.mybir as mybir

K, T, S, J = 1024, 2048, 512, 512
P = 128
PACK = 4
K_PASS = P * PACK
PASSES = K // K_PASS
TILES = J // P
PAIR = 2 * P
PAIRS = J // PAIR
QUADRANTS = 4
QUADRANT = P // QUADRANTS
PLANE_ROWS = 4
SPREAD = QUADRANT // (PASSES * PLANE_ROWS)
LIST_ROWS = 16
SCALE = 4.0
FLOPS = 2 * K * J * S

HEAD = T // 4
TABLE_BYTES = 4 * T
ROW_BYTES = 4 * S

WHOLE = slice(0, S)
FRONT, BACK = slice(0, S // 2), slice(S // 2, S)

F32 = mybir.dt.float32
BF16 = mybir.dt.bfloat16
I32 = mybir.dt.int32
U32 = mybir.dt.uint32
U16 = mybir.dt.uint16
U8 = mybir.dt.uint8
FP8X4 = mybir.dt.float8_e4m3fn_x4
ALU = mybir.AluOpType
ACT = mybir.ActivationFunctionType


def tile_picked_zams_soft_p_kernel(tc, x_words, x_scales, hT, label, offs, out):
    nc = tc.nc
    with ExitStack() as ctx:
        keep = ctx.enter_context(tc.tile_pool(name="keep", bufs=1))
        shared = ctx.enter_context(tc.tile_pool(name="shared", bufs=1))
        psum = ctx.enter_context(tc.psum_pool(name="psum", bufs=1))

        offsets = keep.tile([P, S // LIST_ROWS], U16, name="offsets")
        scale_table = shared.tile([P, T], U8, name="scale_table", offset=TABLE_BYTES - T // 2)
        word_table = [keep.tile([P, T], I32, name="word_table0", align_bytes=64), shared.tile([P, T], I32, name="word_table1", offset=0)]
        h_second = shared.tile([P, PAIRS, PACK, PAIR], F32, name="h_second", offset=TABLE_BYTES)
        h_first = keep.tile([P, PACK, J], F32, name="h_first", tag="first", align_bytes=64)
        x_scales_picked = keep.tile([P, S], U8, name="x_scales_picked", align_bytes=64)
        x_planes = keep.tile([P, PASSES * S], U8, name="x_planes", align_bytes=64)

        nc.vector.memset(scale_table[:].bitcast(I32), 0)
        nc.vector.memset(x_planes[:].bitcast(I32), 0)

        def load_words(o, columns):
            words = x_words[o].rearrange("p n t -> p (n t)").bitcast(I32)
            nc.sync.dma_start(out=word_table[o][:, columns], in_=words[:, columns])

        def h_rows(o):
            return hT[o * K_PASS : (o + 1) * K_PASS, :].rearrange("(p r) c -> p r c", r=PACK)

        load_words(0, slice(0, HEAD))
        nc.sync.dma_start(offsets[:], offs)
        nc.sync.dma_start(out=scale_table[::SPREAD, :].bitcast(I32), in_=x_scales.bitcast(I32).rearrange("o i c -> i o c"))
        load_words(0, slice(HEAD, T))
        nc.sync.dma_start(out=h_first[:], in_=h_rows(0))
        nc.vector.tensor_copy(x_scales_picked[:], scale_table[:].indirect(offsets[:]))
        for q in range(QUADRANTS):
            first = QUADRANT * q
            (nc.sync, nc.scalar)[q % 2].dma_start(
                out=x_planes[first : first + PLANE_ROWS, :].bitcast(I32),
                in_=x_scales_picked[first : first + QUADRANT : SPREAD, :].bitcast(I32),
            )
        load_words(1, slice(0, T))
        for g in range(PAIRS):
            nc.sync.dma_start(out=h_second[:, g], in_=h_rows(1)[:, :, g * PAIR : (g + 1) * PAIR])

        x_codes = [keep.tile([P, S], U32, name="x_codes%d" % o, align_bytes=64) for o in range(PASSES)]
        scores = [psum.tile([P, S], F32, name="scores%d" % m) for m in range(TILES)]
        h_bf16 = [[keep.tile([P, P * PACK], BF16, name="h_bf16_%d_%d" % (o, m), align_bytes=64) for m in range(TILES)] for o in range(PASSES)]
        h_codes = [[keep.tile([P, P], U32, name="h_codes%d_%d" % (o, m), align_bytes=64) for m in range(TILES)] for o in range(PASSES)]
        h_plane = [[keep.tile([P, P], U8, name="h_plane%d_%d" % (o, m), align_bytes=64) for m in range(TILES)] for o in range(PASSES)]
        aside = [(1, FRONT), (3, WHOLE)]
        copied = {
            3: keep.tile([P, S], F32, name="copied3", align_bytes=64),
            1: shared.tile([P, S // 2], F32, name="copied1", offset=TABLE_BYTES),
        }
        differences = {m: keep.tile([P, S], F32, name="difference%d" % m, tag="difference%d" % m, align_bytes=64) for m in (1, 2, 3)}
        differences[0] = shared.tile([P, S], F32, name="difference0", offset=TABLE_BYTES + ROW_BYTES)
        gap = {m: differences[m] for m in (1, 3)}
        gap4 = {m: differences[m] for m in (0, 2)}
        gap4[3] = keep.tile([P, S], F32, name="gap4_3", tag="difference1", align_bytes=64)
        expo = [keep.tile([P, S], F32, name="expo%d" % m) for m in range(TILES)]
        prob = [keep.tile([P, S], F32, name="prob%d" % m) for m in range(TILES)]
        low = {m: keep.tile([P, 1], F32, name="low%d" % m) for m in (0, 1, 3)}
        low[2] = shared.tile([P, 1], F32, name="low2", offset=TABLE_BYTES + ROW_BYTES)
        low_gap = keep.tile([P, 1], F32, name="low_gap")
        total = [keep.tile([P, 1], F32, name="total%d" % m) for m in range(TILES)]
        inv = [keep.tile([P, 1], F32, name="inv%d" % m) for m in range(TILES)]

        def gather_words(o):
            nc.vector.tensor_copy(x_codes[o][:], word_table[o][:].bitcast(U32).indirect(offsets[:]))

        def interleave(o, m):
            if o == 0:
                raw = h_first[:, :, m * P : (m + 1) * P]
            else:
                raw = h_second[:, m // 2, :, (m % 2) * P : (m % 2 + 1) * P]
            dst = h_bf16[o][m][:].rearrange("p (c i r) -> p c r i", i=PACK, r=PACK)
            src = raw.rearrange("p r (c i) -> p c r i", i=PACK)
            if (o, m) == (1, 3):
                nc.vector.tensor_copy(dst, src)
            elif (o, m) == (1, 2):
                nc.scalar.activation(dst, src, ACT.Copy, scale=SCALE)
            elif m % 2 == 0:
                nc.vector.tensor_scalar(dst, src, SCALE, None, ALU.mult)
            else:
                nc.scalar.activation(dst, src, ACT.Copy)

        def quantize(o, m):
            nc.vector.quantize_mx(out=h_codes[o][m][:].bitcast(FP8X4), scales=h_plane[o][m][:], in_=h_bf16[o][m][:])

        def multiply(m, o):
            nc.tensor.matmul_mx(
                out=scores[m][:],
                lhsT=h_codes[o][m][:].bitcast(FP8X4),
                lhsT_scale=h_plane[o][m][:],
                rhs=x_codes[o][:].bitcast(FP8X4),
                rhs_scale=x_planes[:, o * S : (o + 1) * S],
                start=(o == 0),
                stop=(o == PASSES - 1),
            )

        def subtract(m):
            nc.vector.scalar_tensor_tensor(gap4[m][:], margin[:, m, :], SCALE, scores[m][:], ALU.mult, ALU.subtract)

        def minimum(m):
            nc.vector.tensor_reduce(low[m][:], gap4[m][:], mybir.AxisListType.X, ALU.min)

        def scaled_minimum(m):
            nc.vector.tensor_scalar(gap4[m][:], gap[m][:], SCALE, None, ALU.mult, ALU.min, accum_out=low[m][:])

        def exponent(m):
            nc.scalar.activation(expo[m][:], gap4[m][:], ACT.Exp, bias=low[m][:], scale=-1.0, accum_out=total[m][:])

        def invert(m):
            nc.vector.reciprocal(inv[m][:], total[m][:])

        def normalise(m, c):
            nc.vector.tensor_scalar(prob[m][:, c], expo[m][:, c], inv[m][:], None, ALU.mult)

        def normalise_on_gpsimd(m, c):
            nc.gpsimd.tensor_scalar(prob[m][:, c], expo[m][:, c], inv[m][:], 0.0, ALU.mult, ALU.add)

        def store(m, c):
            nc.sync.dma_start(out=out[m * P : (m + 1) * P, c], in_=prob[m][:, c])

        gather_words(0)
        for m in range(TILES):
            interleave(0, m)
        margin = keep.tile([P, TILES, S], F32, name="margin", tag="first", align_bytes=64)
        for m in (0, 1, 3, 2):
            nc.sync.dma_start(out=margin[:, m, :], in_=label[m * P : (m + 1) * P, :])
        for m in range(TILES):
            quantize(0, m)
        for m in range(TILES):
            multiply(m, 0)
        gather_words(1)
        for pair in ((0, 1), (3, 2)):
            for m in pair:
                interleave(1, m)
            for m in pair:
                quantize(1, m)
            for m in pair:
                multiply(m, 1)

        subtract(0)
        for m, c in aside:
            nc.scalar.activation(copied[m][:], scores[m][:, c], ACT.Copy)
            nc.gpsimd.tensor_tensor(gap[m][:, c], margin[:, m, c], copied[m][:], ALU.subtract)
        nc.vector.tensor_tensor(gap[1][:, BACK], margin[:, 1, BACK], scores[1][:, BACK], ALU.subtract)
        minimum(0)
        exponent(0)
        nc.vector.tensor_reduce(low_gap[:], gap[1][:], mybir.AxisListType.X, ALU.min)
        nc.scalar.activation(low[1][:], low_gap[:], ACT.Copy, scale=SCALE)
        nc.scalar.activation(expo[1][:], gap[1][:], ACT.Exp, bias=low[1][:], scale=-SCALE, accum_out=total[1][:])
        subtract(2)

        invert(0)
        normalise_on_gpsimd(0, FRONT)
        nc.scalar.activation(prob[0][:, BACK], expo[0][:, BACK], ACT.Copy, scale=inv[0][:])
        store(0, WHOLE)
        minimum(2)
        exponent(2)
        invert(1)
        normalise_on_gpsimd(1, FRONT)
        store(1, FRONT)
        scaled_minimum(3)
        exponent(3)
        invert(2)
        normalise(1, BACK)
        store(1, BACK)
        normalise(2, WHOLE)
        store(2, WHOLE)
        invert(3)
        for c in (FRONT, BACK):
            normalise(3, c)
            store(3, c)
